import numpy as np
import ml_dtypes


def mxq(x, axis, fmt="e4m3"):
    dtype, down = {"e4m3": (ml_dtypes.float8_e4m3fn, 7), "e5m2": (ml_dtypes.float8_e5m2, 14)}[fmt]
    v = np.moveaxis(np.asarray(x, np.float32).astype(ml_dtypes.bfloat16).astype(np.float64), axis, -1)
    blocks = v.reshape(v.shape[:-1] + (-1, 32))
    amax = np.abs(blocks).max(-1, keepdims=True)
    byte = np.maximum(np.where(amax > 0, np.frexp(amax)[1] - 1 + 127, 0) - down, 1)
    scale = np.exp2(byte - 127.0)
    codes = (blocks / scale).astype(np.float32).astype(dtype).astype(np.float64)
    return np.moveaxis((codes * scale).reshape(v.shape), -1, axis)


WIDE = False


def mx_kscale(k):
    if not WIDE:
        return np.ones(k)
    levels = np.array([10, -10, 5, -5, 0])
    if k % 512:
        return np.exp2(np.random.permutation(np.resize(levels, k // 32))).repeat(32)
    a = np.empty((k // 512, 16))
    for p in range(k // 512):
        a[p, :8] = np.random.permutation(np.resize(levels, 8))
        for g in range(8):
            far = levels[np.abs(levels - a[p, g]) >= 10]
            a[p, g + 8] = far[np.random.randint(len(far))]
    return np.exp2(a.ravel()).repeat(32)


BF16 = ml_dtypes.bfloat16


def bf(x):
    return np.asarray(x, np.float32).astype(BF16)


def f64(x):
    return np.asarray(x).astype(np.float64)


E2M1 = np.array([0.0, 0.5, 1.0, 1.5, 2.0, 3.0, 4.0, 6.0, -0.0, -0.5, -1.0, -1.5, -2.0, -3.0, -4.0, -6.0])


def pack_weight(w, fmt):
    k, n = w.shape
    w = f64(bf(w)).reshape(k // 32, 32, n)
    amax = np.abs(w).max(1)
    if fmt == "e4m3":
        byte = np.frexp(amax)[1] - 1 + 127 - 7
    else:
        mant, ex = np.frexp(amax / 6.0)
        byte = np.where(mant > 0.5, ex, ex - 1) + 127
    byte = np.clip(np.where(amax > 0, byte, 1), 1, 254)
    scaled = (w * np.exp2(127.0 - byte)[:, None, :]).reshape(k, n).astype(np.float32)
    by_word = np.ascontiguousarray(scaled.reshape(k // 512, 128, 4, n).transpose(0, 1, 3, 2))
    if fmt == "e4m3":
        words = by_word.astype(ml_dtypes.float8_e4m3fn).view(np.uint8)
    else:
        c = by_word.astype(ml_dtypes.float4_e2m1fn).view(np.uint8) & 0xF
        words = c[..., 0::2] | (c[..., 1::2] << 4)
    return np.ascontiguousarray(words), np.ascontiguousarray(byte.astype(np.uint8).reshape(k // 512, 16, n))


def unpack_weight(words, scales, fmt):
    g, p, n, _ = words.shape
    if fmt == "e4m3":
        vals = np.ascontiguousarray(words).view(ml_dtypes.float8_e4m3fn).astype(np.float64)
    else:
        nib = np.empty((g, p, n, 4), np.uint8)
        nib[..., 0::2] = words & 0xF
        nib[..., 1::2] = words >> 4
        vals = E2M1[nib]
    vals = vals * np.repeat(np.exp2(scales.astype(np.float64) - 127.0), 8, axis=1)[..., None]
    return vals.transpose(0, 1, 3, 2).reshape(g * 512, n)

def planes(Y):
    n, m = Y.shape
    b = f64(bf(Y)).reshape(n // 32, 32, m)
    amax = np.abs(b).max(1)
    byte = np.clip(np.where(amax > 0, np.frexp(amax)[1] - 1 + 127 - 7, 1), 1, 254)
    codes = (b * np.exp2(127.0 - byte)[:, None, :]).reshape(n, m).astype(np.float32).astype(ml_dtypes.float8_e4m3fn).view(np.uint8)
    words = codes.reshape(n // 512, 128, 4, m).transpose(0, 1, 3, 2)
    return np.ascontiguousarray(words), np.ascontiguousarray(byte.astype(np.uint8).reshape(n // 512, 16, m))


B, N, D, A, F, C = 4, 512, 1024, 256, 1024, 128


def sigmoid(v):
    return 1.0 / (1.0 + np.exp(-v))


def softmax(v, axis):
    ex = np.exp(v - v.max(axis=axis, keepdims=True))
    return ex / ex.sum(axis=axis, keepdims=True)


def setup_inputs():
    s, t = mx_kscale(D), mx_kscale(F)
    h = bf(np.random.standard_normal((B, N, D)) * s)
    wv_words, wv_scales = pack_weight(np.random.standard_normal((D, A)) / np.sqrt(D) / s[:, None], "e4m3")
    wu_words, wu_scales = pack_weight(np.random.standard_normal((D, A)) / np.sqrt(D) / s[:, None], "e4m3")
    wa = bf(3.0 * np.random.standard_normal(A) / np.sqrt(A))
    w1_words, w1_scales = pack_weight(np.random.standard_normal((D, F)) / np.sqrt(D) / s[:, None] * t, "e4m3")
    b1 = bf(0.3 * np.random.standard_normal(F) * t)
    w2_words, w2_scales = pack_weight(np.random.standard_normal((F, C)) / np.sqrt(F) / t[:, None], "e4m3")
    return {"h": h,
            "wv_words": wv_words, "wv_scales": wv_scales,
            "wu_words": wu_words, "wu_scales": wu_scales,
            "wa": wa,
            "w1_words": w1_words, "w1_scales": w1_scales,
            "b1": b1,
            "w2_words": w2_words, "w2_scales": w2_scales}


def gated_attention_scores(hq, wv_words, wv_scales, wu_words, wu_scales, wa):
    v = hq @ unpack_weight(wv_words, wv_scales, "e4m3")
    u = hq @ unpack_weight(wu_words, wu_scales, "e4m3")
    return np.sum(np.tanh(v) * sigmoid(u) * f64(wa), axis=-1)


def core(h, wv_words, wv_scales, wu_words, wu_scales, wa, w1_words, w1_scales, b1, w2_words, w2_scales):
    n_patches = h.shape[1]
    hq = mxq(f64(h), 2, "e4m3")
    e = gated_attention_scores(hq, wv_words, wv_scales, wu_words, wu_scales, wa)
    a = n_patches * softmax(e, 1)
    z = hq @ unpack_weight(w1_words, w1_scales, "e4m3")
    p = np.maximum(a[:, :, None] * z + f64(b1), 0.0)
    return mxq(p, 2, "e4m3") @ unpack_weight(w2_words, w2_scales, "e4m3")


def reference(h, wv_words, wv_scales, wu_words, wu_scales, wa, w1_words, w1_scales, b1, w2_words, w2_scales):
    R_out = core(h, wv_words, wv_scales, wu_words, wu_scales, wa, w1_words, w1_scales, b1, w2_words, w2_scales)
    words, scales = planes(np.moveaxis(R_out, 1, 0).reshape(512, -1))
    return R_out, words, scales

@@ -1,0 +1,368 @@
+from contextlib import ExitStack
+
+import concourse.mybir as mybir
+from concourse.masks import make_identity
+
+B, N, D, A, F, C = 4, 512, 1024, 256, 1024, 128
+FLOPS = 2 * B * N * (2 * D * A + D * F + F * C)
+
+F32 = mybir.dt.float32
+BF16 = mybir.dt.bfloat16
+I32 = mybir.dt.int32
+U32 = mybir.dt.uint32
+U8 = mybir.dt.uint8
+FP8X4 = mybir.dt.float8_e4m3fn_x4
+ACT = mybir.ActivationFunctionType
+ALU = mybir.AluOpType
+AXIS = mybir.AxisListType
+
+P = 128
+PACK = 4
+PASSES = 2
+BANK = 512
+TILES = B * PACK
+PAIRS = TILES // 2
+ROTATING_BANKS = 8
+RELU_ON_VECTOR = (13, 15)
+
+
+def tile_additivemilpatchcontributionlogits_x2_kernel(
+    tc, h, wv_words, wv_scales, wu_words, wu_scales, wa, w1_words, w1_scales, b1, w2_words, w2_scales,
+    out_0, out_1, out_2,
+):
+    nc = tc.nc
+    with ExitStack() as ctx:
+        keep = ctx.enter_context(tc.tile_pool(name="keep", bufs=1))
+        work = ctx.enter_context(tc.tile_pool(name="work", bufs=4))
+        psum = ctx.enter_context(tc.psum_pool(name="psum", bufs=1))
+        ctx.enter_context(tc.manual_schedule(engines={mybir.EngineType.PE, mybir.EngineType.SP}))
+
+        banks_taken = []
+
+        def next_bank():
+            k = len(banks_taken) % ROTATING_BANKS
+            banks_taken.append(k)
+            return psum.tile([P, BANK], F32, name="bank%d" % k)
+
+        def weight_tiles(name, width):
+            codes = keep.tile([P, PASSES, width], U32, name=name + "_codes", align_bytes=64)
+            scales = keep.tile([P, PASSES, width], U8, name=name + "_scales", align_bytes=64)
+            nc.vector.memset(scales[:].bitcast(I32), 0)
+            return codes, scales
+
+        def load_codes(codes, words, g0, g1):
+            src = words.rearrange("g p n t -> p g (n t)").bitcast(I32)
+            nc.sync.dma_start(out=codes[:, g0:g1, :].bitcast(I32), in_=src[:, g0:g1, :])
+
+        def load_scales(queue, scales, rows):
+            for q in range(4):
+                queue.dma_start(
+                    out=scales[32 * q : 32 * q + 4, :, :].bitcast(I32),
+                    in_=rows[:, 4 * q : 4 * q + 4, :].rearrange("g r n -> r g n").bitcast(I32),
+                )
+
+        h_raw = [keep.tile([P, PACK, D], BF16, name="h_raw%d" % b) for b in range(B)]
+
+        def load_h(b, t0, t1):
+            nc.sync.dma_start(out=h_raw[b][:, t0:t1, :], in_=h[b].rearrange("(p t) d -> p t d", t=PACK)[:, t0:t1, :])
+
+        ident = keep.tile([P, P], F32)
+        make_identity(nc, ident[:])
+        wu_c, wu_s = weight_tiles("wu", A)
+        wv_c, wv_s = weight_tiles("wv", A)
+        zeros = keep.tile([P, P], BF16)
+        nc.vector.memset(zeros[:], 0.0)
+        wa_row = keep.tile([P, A], BF16)
+        nc.vector.memset(wa_row[:], 0.0)
+        b1_row = keep.tile([P, F], BF16)
+        nc.vector.memset(b1_row[:], 0.0)
+        w1_c, w1_s = weight_tiles("w1", F)
+        w2_c, w2_s = weight_tiles("w2", C)
+
+        load_h(0, 0, 1)
+        load_h(0, 1, 2)
+        load_h(0, 2, 4)
+        load_scales(nc.scalar, wu_s, wu_scales)
+        load_codes(wu_c, wu_words, 0, 2)
+        load_codes(wv_c, wv_words, 0, 2)
+        load_scales(nc.scalar, wv_s, wv_scales)
+        ones = keep.tile([P, P], BF16)
+        nc.scalar.activation(out=ones[:], in_=zeros[:], func=ACT.Exp)
+        nc.gpsimd.dma_start(out=wa_row[0:1, :], in_=wa.unsqueeze(0))
+        nc.gpsimd.dma_start(out=b1_row[0:1, :], in_=b1.unsqueeze(0))
+        for j in range(2, PAIRS):
+            load_h(j // 2, 2 * (j % 2), 2 * (j % 2) + 2)
+        load_scales(nc.sync, w1_s, w1_scales)
+        load_scales(nc.sync, w2_s, w2_scales)
+        load_codes(w1_c, w1_words, 0, 1)
+        load_codes(w1_c, w1_words, 1, 2)
+        load_codes(w2_c, w2_words, 0, 2)
+
+        wa_all = keep.tile([P, A], F32)
+        b1_all = keep.tile([P, PASSES, 2, P, 2], F32)
+        h_codes = [keep.tile([P, PASSES * P], U32, name="h_codes%d" % i, align_bytes=64) for i in range(TILES)]
+        h_scales = [keep.tile([P, PASSES * P], U8, name="h_scales%d" % i, align_bytes=64) for i in range(TILES)]
+        neg_e = [keep.tile([P, PACK], F32, name="neg_e%d" % b) for b in range(B)]
+        expo = [keep.tile([P, PACK], F32, name="expo%d" % b) for b in range(B)]
+        attn = [keep.tile([P, PACK], F32, name="attn%d" % b) for b in range(B)]
+        part_min = [keep.tile([P, 1], F32, name="part_min%d" % b) for b in range(B)]
+        part_sum = [keep.tile([P, 1], F32, name="part_sum%d" % b) for b in range(B)]
+        out_codes = keep.tile([P, B * C], U32, align_bytes=64)
+        out_scales = keep.tile([P, B * C], U8, align_bytes=64)
+        held = {}
+
+        def spread_wa():
+            bank = next_bank()
+            nc.tensor.matmul(bank[:, 0:A], lhsT=ones[:], rhs=wa_row[:], start=True, stop=True)
+            nc.vector.tensor_copy(out=wa_all[:], in_=bank[:, 0:A])
+
+        def spread_b1(half):
+            bank = next_bank()
+            nc.tensor.matmul(bank[:], lhsT=ones[:], rhs=b1_row[:, half * BANK : (half + 1) * BANK], start=True, stop=True)
+            nc.vector.tensor_copy(out=b1_all[:, half], in_=bank[:].rearrange("p (m u e) -> p u m e", u=2, e=2))
+
+        def h_turn(i):
+            words = h_raw[i // PACK][:, i % PACK, :].bitcast(F32)
+            bank = next_bank()
+            for u in range(2):
+                for g in range(PASSES):
+                    col = (u * PASSES + g) * P
+                    nc.tensor.transpose(bank[:, col : col + P], words[:, 256 * g + u : 256 * (g + 1) : 2], ident[:])
+            held["h_bank", i] = bank
+
+        def h_copy(i):
+            grouped = work.tile([P, D], BF16, name="h_grouped", align_bytes=64)
+            nc.scalar.copy(
+                out=grouped[:].bitcast(F32).rearrange("p (q u) -> p q u", u=2),
+                in_=held["h_bank", i][:].rearrange("p (u q) -> p q u", u=2),
+            )
+            held["h_grouped", i] = grouped
+
+        def h_quant(i):
+            nc.vector.quantize_mx(out=h_codes[i][:].bitcast(FP8X4), scales=h_scales[i][:], in_=held["h_grouped", i][:])
+
+        def times_h(out, i, codes, scales, cols):
+            for g in range(PASSES):
+                k = slice(g * P, (g + 1) * P)
+                nc.tensor.matmul_mx(
+                    out=out, lhsT=h_codes[i][:, k].bitcast(FP8X4), lhsT_scale=h_scales[i][:, k],
+                    rhs=codes[:, g, cols].bitcast(FP8X4), rhs_scale=scales[:, g, cols],
+                    start=(g == 0), stop=(g == PASSES - 1),
+                )
+
+        def gate_matmul(j, key, codes, scales):
+            bank = next_bank()
+            for s in range(2):
+                times_h(bank[:, s * A : (s + 1) * A], 2 * j + s, codes, scales, slice(0, A))
+            held[key, j] = bank
+
+        def u_matmul(j):
+            gate_matmul(j, "u_bank", wu_c, wu_s)
+
+        def v_matmul(j):
+            gate_matmul(j, "v_bank", wv_c, wv_s)
+
+        def u_tanh(j):
+            tanh_u = work.tile([P, 2, A], F32, name="tanh_u")
+            nc.scalar.activation(out=tanh_u[:].rearrange("p s a -> p (s a)"), in_=held["u_bank", j][:], func=ACT.Tanh, scale=0.5)
+            held["tanh_u", j] = tanh_u
+
+        def v_tanh(j):
+            tanh_v = work.tile([P, 2, A], F32, name="tanh_v")
+            nc.scalar.activation(out=tanh_v[:].rearrange("p s a -> p (s a)"), in_=held["v_bank", j][:], func=ACT.Tanh)
+            held["tanh_v", j] = tanh_v
+
+        def gate_weigh(j):
+            gate = work.tile([P, 2, A], F32, name="gate")
+            nc.vector.scalar_tensor_tensor(
+                out=gate[:], in0=held["tanh_u", j][:], scalar=1.0,
+                in1=wa_all[:].unsqueeze(1).to_broadcast([P, 2, A]), op0=ALU.add, op1=ALU.mult,
+            )
+            held["gate", j] = gate
+
+        def score(i):
+            terms = work.tile([P, A], F32, name="terms")
+            b, t = divmod(i, PACK)
+            nc.vector.scalar_tensor_tensor(
+                out=terms[:], in0=held["tanh_v", i // 2][:, i % 2, :], scalar=-0.5,
+                in1=held["gate", i // 2][:, i % 2, :], op0=ALU.mult, op1=ALU.mult,
+                accum_out=neg_e[b][:, t : t + 1],
+            )
+
+        def min_local(b):
+            nc.vector.tensor_reduce(out=part_min[b][:], in_=neg_e[b][:], axis=AXIS.X, op=ALU.min)
+
+        def spread_column(column):
+            bank = next_bank()
+            nc.tensor.transpose(bank[:, 0:P], column.to_broadcast([P, P]), ident[:])
+            return bank
+
+        def min_spread(b):
+            held["min_bank", b] = spread_column(part_min[b][:])
+
+        def min_all(b):
+            bag_min = work.tile([P, 1], F32, name="bag_min")
+            nc.vector.tensor_reduce(out=bag_min[:], in_=held["min_bank", b][:, 0:P], axis=AXIS.X, op=ALU.min)
+            held["bag_min", b] = bag_min
+
+        def exponent(b):
+            nc.scalar.activation(
+                out=expo[b][:], in_=neg_e[b][:], func=ACT.Exp, scale=-1.0, bias=held["bag_min", b][:],
+                accum_out=part_sum[b][:],
+            )
+
+        def sum_spread(b):
+            held["sum_bank", b] = spread_column(part_sum[b][:])
+
+        def sum_all(b):
+            total = work.tile([P, 1], F32, name="total")
+            nc.vector.tensor_reduce(out=total[:], in_=held["sum_bank", b][:, 0:P], axis=AXIS.X, op=ALU.add)
+            held["total", b] = total
+
+        def invert(b):
+            inverse = work.tile([P, 1], F32, name="inverse")
+            nc.vector.reciprocal(out=inverse[:], in_=held["total", b][:])
+            held["inverse", b] = inverse
+
+        def normalise(b):
+            nc.vector.tensor_scalar(
+                out=attn[b][:], in0=expo[b][:], scalar1=held["inverse", b][:], scalar2=float(N), op0=ALU.mult, op1=ALU.mult
+            )
+
+        def z_matmul(i, half):
+            bank = next_bank()
+            times_h(bank[:], i, w1_c, w1_s, slice(half * BANK, (half + 1) * BANK))
+            held["z_bank", i, half] = bank
+
+        def z_affine(i, half):
+            if half == 0:
+                held["pre", i] = work.tile([P, PASSES, 2, P, 2], BF16, name="pre", bufs=8)
+            b, t = divmod(i, PACK)
+            z = held["z_bank", i, half][:].rearrange("p (m u e) -> p u m e", u=2, e=2)
+            for u in range(2):
+                nc.vector.scalar_tensor_tensor(
+                    out=held["pre", i][:, half, u], in0=z[:, u], scalar=attn[b][:, t : t + 1],
+                    in1=b1_all[:, half, u], op0=ALU.mult, op1=ALU.add,
+                )
+
+        def p_turn(i):
+            words = held["pre", i][:].rearrange("p g u m e -> p (g u m e)").bitcast(F32)
+            bank = next_bank()
+            for g in range(PASSES):
+                for u in range(2):
+                    src, col = (g * 2 + u) * P, (u * PASSES + g) * P
+                    nc.tensor.transpose(bank[:, col : col + P], words[:, src : src + P], ident[:])
+            held["p_bank", i] = bank
+
+        def p_relu(i):
+            grouped = work.tile([P, F], BF16, name="p_grouped", align_bytes=64)
+            dst = grouped[:].rearrange("p (q u e) -> p q u e", u=2, e=2)
+            src = held["p_bank", i][:].bitcast(BF16).rearrange("p (u q e) -> p q u e", u=2, e=2)
+            if i in RELU_ON_VECTOR:
+                nc.vector.tensor_scalar(out=dst, in0=src, scalar1=0.0, scalar2=None, op0=ALU.max)
+            else:
+                nc.scalar.activation(out=dst, in_=src, func=ACT.Relu)
+            held["p_grouped", i] = grouped
+
+        def p_quant(i):
+            codes = work.tile([P, PASSES * P], U32, name="p_codes", align_bytes=64, bufs=8)
+            scales = work.tile([P, PASSES * P], U8, name="p_scales", align_bytes=64, bufs=8)
+            nc.vector.quantize_mx(out=codes[:].bitcast(FP8X4), scales=scales[:], in_=held["p_grouped", i][:])
+            held["p_quant", i] = (codes, scales)
+
+        def out_matmul(i):
+            b, t = divmod(i, PACK)
+            if t == 0:
+                held["out_bank", b] = next_bank()
+            codes, scales = held["p_quant", i]
+            for g in range(PASSES):
+                k = slice(g * P, (g + 1) * P)
+                nc.tensor.matmul_mx(
+                    out=held["out_bank", b][:, t * C : (t + 1) * C],
+                    lhsT=codes[:, k].bitcast(FP8X4), lhsT_scale=scales[:, k],
+                    rhs=w2_c[:, g, :].bitcast(FP8X4), rhs_scale=w2_s[:, g, :],
+                    start=(g == 0), stop=(g == PASSES - 1),
+                )
+
+        def out_copy(b):
+            result = work.tile([P, PACK * C], F32, name="result")
+            nc.scalar.copy(out=result[:], in_=held["out_bank", b][:])
+            nc.sync.dma_start(out=out_0[b].rearrange("(p t) c -> p (t c)", t=PACK), in_=result[:])
+            held["result", b] = result
+
+        def out_round(b):
+            grouped = work.tile([P, C, PACK], BF16, name="out_grouped", align_bytes=64)
+            if b == B - 1:
+                nc.vector.tensor_copy(out=grouped[:], in_=held["result", b][:].rearrange("p (t c) -> p c t", t=PACK))
+            else:
+                nc.scalar.copy(out=grouped[:], in_=held["out_bank", b][:].rearrange("p (t c) -> p c t", t=PACK))
+            held["out_grouped", b] = grouped
+
+        def out_quant(b):
+            cols = slice(b * C, (b + 1) * C)
+            nc.vector.quantize_mx(
+                out=out_codes[:, cols].bitcast(FP8X4), scales=out_scales[:, cols],
+                in_=held["out_grouped", b][:].rearrange("p c t -> p (c t)"),
+            )
+            nc.sync.dma_start(
+                out=out_1[0].rearrange("p m t -> p (m t)").bitcast(I32)[:, cols], in_=out_codes[:, cols].bitcast(I32)
+            )
+
+        def store_scales():
+            for q in range(4):
+                queue = nc.sync if q % 2 == 0 else nc.scalar
+                queue.dma_start(
+                    out=out_2[0, 4 * q : 4 * q + 4, :].bitcast(I32), in_=out_scales[32 * q : 32 * q + 4, :].bitcast(I32)
+                )
+
+        H_ROUNDS = [range(0, 2), range(2, 6), range(6, 10), range(10, 14), range(14, 16)]
+        Z_ROUNDS = [range(0, 4), range(4, 8), range(8, 12), range(12, 14), range(14, 16)]
+        Z_FIRST = len(H_ROUNDS)
+
+        def of_round(rounds, r):
+            return rounds[r] if 0 <= r < len(rounds) else range(0)
+
+        for r in range(Z_FIRST + len(Z_ROUNDS) + 2):
+            if 0 <= r - 4 < B:
+                min_spread(r - 4)
+                min_all(r - 4)
+                exponent(r - 4)
+            if 0 <= r - 5 < B:
+                sum_spread(r - 5)
+                sum_all(r - 5)
+                invert(r - 5)
+                normalise(r - 5)
+            for i in of_round(H_ROUNDS, r):
+                h_turn(i)
+                h_copy(i)
+                h_quant(i)
+            for i in of_round(Z_ROUNDS, r - Z_FIRST - 1):
+                p_turn(i)
+                p_relu(i)
+                p_quant(i)
+            if r == 0:
+                spread_wa()
+            for j in [i // 2 for i in of_round(H_ROUNDS, r - 1) if i % 2 == 1]:
+                u_matmul(j)
+                u_tanh(j)
+                v_matmul(j)
+                v_tanh(j)
+                gate_weigh(j)
+                score(2 * j)
+                score(2 * j + 1)
+                if j % 2 == 1:
+                    min_local(j // 2)
+            if r == 1:
+                spread_b1(0)
+                spread_b1(1)
+            for i in of_round(Z_ROUNDS, r - Z_FIRST):
+                for half in range(2):
+                    z_matmul(i, half)
+                    z_affine(i, half)
+            for i in of_round(Z_ROUNDS, r - Z_FIRST - 2):
+                out_matmul(i)
+                if i % PACK == PACK - 1:
+                    out_copy(i // PACK)
+                    out_round(i // PACK)
+                    out_quant(i // PACK)
+        store_scales()

@@ -23,7 +23,42 @@ BANK = 512
 TILES = B * PACK
 PAIRS = TILES // 2
 ROTATING_BANKS = 8
-RELU_ON_VECTOR = (13, 15)
+RELU_ON_VECTOR = ()
+LAST_RELU_ON_VECTOR = ()
+H_COPY_ON_VECTOR = (2,)
+ROUND_ON_VECTOR = (1, 3, 2,)
+GATE_ON_GPSIMD = ()
+ORDER = [
+    ("HT", 0), ("HT", 1), ("HC", 0), ("HT", 2), ("HC", 1), ("HT", 3), ("HQ", 0), ("BC", 0), ("HC", 2),
+    ("HC", 3), ("UU", 0), ("BCs", 0), ("VV", 0), ("TU", 0), ("HQ", 1), ("HT", 4), ("TV", 0), ("G1", 0),
+    ("HT", 5), ("HC", 4), ("HT", 6), ("G2", 0), ("HC", 5), ("HT", 7), ("G2", 1), ("HC", 6), ("BC", 1),
+    ("HQ", 2), ("UU", 1), ("HC", 7), ("BCs", 1), ("BC", 2), ("VV", 1), ("TU", 1), ("HQ", 3), ("UU", 2),
+    ("G1", 1), ("TV", 1), ("UU", 3), ("BCs", 2), ("TU", 2), ("HT", 8), ("G2", 2), ("TU", 3), ("HT", 9),
+    ("G2", 3), ("HC", 8), ("G1", 2), ("VV", 2), ("HC", 9), ("VV", 3), ("G1", 3), ("TV", 2), ("HQ", 4),
+    ("HT", 10), ("TV", 3), ("HT", 11), ("G2", 4), ("HC", 10), ("G2", 5), ("UU", 4), ("G2", 6), ("HC", 11),
+    ("VV", 4), ("G2", 7), ("TU", 4), ("HT", 12), ("HQ", 5), ("TV", 4), ("HT", 13), ("M4", 0), ("G1", 4),
+    ("HC", 12), ("EA", 0), ("UU", 5), ("HC", 13), ("MX", 0), ("G2", 8), ("HT", 14), ("EX", 0), ("EX", 1),
+    ("G2", 9), ("TU", 5), ("EB", 0), ("HQ", 6), ("Z", 0), ("HC", 14), ("VV", 5), ("RC", 0), ("G1", 5),
+    ("AM", 0), ("AM", 1), ("Z", 1), ("ZE", 0), ("TV", 5), ("HT", 15), ("ZE", 1), ("UU", 6), ("HC", 15),
+    ("G2", 10), ("Z", 2), ("G2", 11), ("TU", 6), ("Z", 3), ("HQ", 7), ("PT", 0), ("ZE", 2), ("Z", 4),
+    ("PR", 0), ("ZE", 3), ("Z", 5), ("ZE", 4), ("Z", 6), ("Z", 7), ("ZE", 5), ("VV", 6), ("ZE", 6), ("Z", 8),
+    ("TV", 6), ("ZE", 7), ("UU", 7), ("ZE", 8), ("VV", 7), ("TU", 7), ("G1", 6), ("PT", 1), ("TV", 7),
+    ("PT", 2), ("G1", 7), ("Z", 9), ("PR", 1), ("G2", 12), ("PT", 3), ("G2", 13), ("Z", 10), ("PR", 2),
+    ("ZE", 9), ("ZE", 10), ("PT", 4), ("PR", 3), ("Z", 11), ("G2", 14), ("G2", 15), ("Z", 12), ("PR", 4),
+    ("ZE", 11), ("Z", 13), ("M4", 1), ("ZE", 12), ("EA", 1), ("Z", 14), ("ZE", 13), ("Z", 15), ("MX", 1),
+    ("Z", 16), ("ZE", 14), ("EX", 2), ("EX", 3), ("PT", 5), ("ZE", 15), ("PT", 6), ("PR", 5), ("EB", 1),
+    ("PQ", 0), ("Z", 17), ("RC", 1), ("Z", 18), ("PQ", 1), ("AM", 2), ("AM", 3), ("PR", 6), ("PT", 7),
+    ("ZE", 16), ("Z", 19), ("ZE", 17), ("PR", 7), ("O", 0), ("O", 1), ("O", 2), ("ZE", 18), ("Z", 20),
+    ("Z", 21), ("ZE", 19), ("Z", 22), ("ZE", 20), ("O", 3), ("Z", 23), ("ZE", 21), ("OC", 0), ("PT", 8),
+    ("ZE", 22), ("PT", 9), ("OB", 0), ("PT", 10), ("ZE", 23), ("PR", 8), ("Z", 24), ("PQ", 2), ("Z", 25),
+    ("PR", 9), ("ZE", 24), ("Z", 26), ("Z", 27), ("ZE", 25), ("PR", 10), ("PT", 11), ("ZE", 26), ("Z", 28),
+    ("ZE", 27), ("PR", 11), ("PT", 12), ("ZE", 28), ("Z", 29), ("PR", 12), ("Z", 30), ("PQ", 3), ("PT", 13),
+    ("ZE", 29), ("O", 4), ("PR", 13), ("ZE", 30), ("PT", 14), ("O", 5), ("PQ", 4), ("O", 6), ("Z", 31),
+    ("PR", 14), ("PQ", 5), ("PTh", 0), ("O", 7), ("ZE", 31), ("O", 8), ("PRh", 0), ("PQ", 6), ("OC", 1),
+    ("PTh", 1), ("O", 9), ("O", 10), ("PQ1", 14), ("PRh", 1), ("O", 11), ("O", 12), ("PQh", 0), ("O", 13),
+    ("OB", 1), ("O", 14), ("OC", 2), ("Oh", 0), ("PQh", 1), ("OQ", 0), ("OCa", 0), ("Oh", 1), ("OQ", 1),
+    ("OB", 2), ("OCb", 0), ("OB", 3), ("OQ", 2), ("OQ", 3),
+]
 
 
 def tile_additivemilpatchcontributionlogits_x2_kernel(
@@ -35,7 +70,7 @@ def tile_additivemilpatchcontributionlogits_x2_kernel(
         keep = ctx.enter_context(tc.tile_pool(name="keep", bufs=1))
         work = ctx.enter_context(tc.tile_pool(name="work", bufs=4))
         psum = ctx.enter_context(tc.psum_pool(name="psum", bufs=1))
-        ctx.enter_context(tc.manual_schedule(engines={mybir.EngineType.PE, mybir.EngineType.SP}))
+        ctx.enter_context(tc.manual_schedule(engines={mybir.EngineType.PE, mybir.EngineType.SP, mybir.EngineType.Activation, mybir.EngineType.DVE}))
 
         banks_taken = []
 
@@ -79,17 +114,19 @@ def tile_additivemilpatchcontributionlogits_x2_kernel(
         w1_c, w1_s = weight_tiles("w1", F)
         w2_c, w2_s = weight_tiles("w2", C)
 
+        ones = keep.tile([P, P], BF16)
+        nc.scalar.activation(out=ones[:], in_=zeros[:], func=ACT.Exp)
+        per_patch = keep.tile([P, P], F32)
+        nc.gpsimd.memset(per_patch[:], 1.0 / N)
+        nc.gpsimd.dma_start(out=wa_row[0:1, :], in_=wa.unsqueeze(0))
+        nc.gpsimd.dma_start(out=b1_row[0:1, :], in_=b1.unsqueeze(0))
         load_h(0, 0, 1)
         load_h(0, 1, 2)
         load_h(0, 2, 4)
-        load_scales(nc.scalar, wu_s, wu_scales)
+        load_scales(nc.sync, wu_s, wu_scales)
         load_codes(wu_c, wu_words, 0, 2)
+        load_scales(nc.sync, wv_s, wv_scales)
         load_codes(wv_c, wv_words, 0, 2)
-        load_scales(nc.scalar, wv_s, wv_scales)
-        ones = keep.tile([P, P], BF16)
-        nc.scalar.activation(out=ones[:], in_=zeros[:], func=ACT.Exp)
-        nc.gpsimd.dma_start(out=wa_row[0:1, :], in_=wa.unsqueeze(0))
-        nc.gpsimd.dma_start(out=b1_row[0:1, :], in_=b1.unsqueeze(0))
         for j in range(2, PAIRS):
             load_h(j // 2, 2 * (j % 2), 2 * (j % 2) + 2)
         load_scales(nc.sync, w1_s, w1_scales)
@@ -100,26 +137,31 @@ def tile_additivemilpatchcontributionlogits_x2_kernel(
 
         wa_all = keep.tile([P, A], F32)
         b1_all = keep.tile([P, PASSES, 2, P, 2], F32)
-        h_codes = [keep.tile([P, PASSES * P], U32, name="h_codes%d" % i, align_bytes=64) for i in range(TILES)]
-        h_scales = [keep.tile([P, PASSES * P], U8, name="h_scales%d" % i, align_bytes=64) for i in range(TILES)]
-        neg_e = [keep.tile([P, PACK], F32, name="neg_e%d" % b) for b in range(B)]
+        h_codes = [keep.tile([P, 2, PASSES * P], U32, name="h_codes%d" % j, align_bytes=64) for j in range(PAIRS)]
+        h_scales = [keep.tile([P, 2, PASSES * P], U8, name="h_scales%d" % j, align_bytes=64) for j in range(PAIRS)]
+        neg_e = [keep.tile([P, 2, PACK], F32, name="neg_e%d" % k) for k in range(B // 2)]
+        part_min = [keep.tile([P, 2], F32, name="part_min%d" % k) for k in range(B // 2)]
+        bag_min = [keep.tile([P, 2], F32, name="bag_min%d" % k) for k in range(B // 2)]
+        part_sum = [keep.tile([P, 2], F32, name="part_sum%d" % k) for k in range(B // 2)]
+        inverse = [keep.tile([P, 2], F32, name="inverse%d" % k) for k in range(B // 2)]
         expo = [keep.tile([P, PACK], F32, name="expo%d" % b) for b in range(B)]
         attn = [keep.tile([P, PACK], F32, name="attn%d" % b) for b in range(B)]
-        part_min = [keep.tile([P, 1], F32, name="part_min%d" % b) for b in range(B)]
-        part_sum = [keep.tile([P, 1], F32, name="part_sum%d" % b) for b in range(B)]
         out_codes = keep.tile([P, B * C], U32, align_bytes=64)
         out_scales = keep.tile([P, B * C], U8, align_bytes=64)
         held = {}
 
-        def spread_wa():
+        def spread_matmul(k):
             bank = next_bank()
-            nc.tensor.matmul(bank[:, 0:A], lhsT=ones[:], rhs=wa_row[:], start=True, stop=True)
-            nc.vector.tensor_copy(out=wa_all[:], in_=bank[:, 0:A])
+            row = wa_row[:] if k == 0 else b1_row[:, (k - 1) * BANK : k * BANK]
+            nc.tensor.matmul(bank[:, 0 : row.shape[1]], lhsT=ones[:], rhs=row, start=True, stop=True)
+            held["row_bank", k] = bank
 
-        def spread_b1(half):
-            bank = next_bank()
-            nc.tensor.matmul(bank[:], lhsT=ones[:], rhs=b1_row[:, half * BANK : (half + 1) * BANK], start=True, stop=True)
-            nc.vector.tensor_copy(out=b1_all[:, half], in_=bank[:].rearrange("p (m u e) -> p u m e", u=2, e=2))
+        def spread_copy(k):
+            bank = held["row_bank", k]
+            if k == 0:
+                nc.vector.tensor_copy(out=wa_all[:], in_=bank[:, 0:A])
+            else:
+                nc.vector.tensor_copy(out=b1_all[:, k - 1], in_=bank[:].rearrange("p (m u e) -> p u m e", u=2, e=2))
 
         def h_turn(i):
             words = h_raw[i // PACK][:, i % PACK, :].bitcast(F32)
@@ -131,21 +173,27 @@ def tile_additivemilpatchcontributionlogits_x2_kernel(
             held["h_bank", i] = bank
 
         def h_copy(i):
-            grouped = work.tile([P, D], BF16, name="h_grouped", align_bytes=64)
-            nc.scalar.copy(
-                out=grouped[:].bitcast(F32).rearrange("p (q u) -> p q u", u=2),
-                in_=held["h_bank", i][:].rearrange("p (u q) -> p q u", u=2),
-            )
-            held["h_grouped", i] = grouped
+            if i % 2 == 0:
+                held["h_grouped", i // 2] = work.tile([P, 2, D], BF16, name="h_grouped", align_bytes=64)
+            dst = held["h_grouped", i // 2][:, i % 2, :].bitcast(F32).rearrange("p (q u) -> p q u", u=2)
+            src = held["h_bank", i][:].rearrange("p (u q) -> p q u", u=2)
+            if i in H_COPY_ON_VECTOR:
+                nc.vector.tensor_copy(out=dst, in_=src)
+            else:
+                nc.scalar.copy(out=dst, in_=src)
 
-        def h_quant(i):
-            nc.vector.quantize_mx(out=h_codes[i][:].bitcast(FP8X4), scales=h_scales[i][:], in_=held["h_grouped", i][:])
+        def h_quant(j):
+            nc.vector.quantize_mx(
+                out=h_codes[j][:].rearrange("p s q -> p (s q)").bitcast(FP8X4),
+                scales=h_scales[j][:].rearrange("p s q -> p (s q)"),
+                in_=held["h_grouped", j][:].rearrange("p s d -> p (s d)"),
+            )
 
         def times_h(out, i, codes, scales, cols):
             for g in range(PASSES):
                 k = slice(g * P, (g + 1) * P)
                 nc.tensor.matmul_mx(
-                    out=out, lhsT=h_codes[i][:, k].bitcast(FP8X4), lhsT_scale=h_scales[i][:, k],
+                    out=out, lhsT=h_codes[i // 2][:, i % 2, k].bitcast(FP8X4), lhsT_scale=h_scales[i // 2][:, i % 2, k],
                     rhs=codes[:, g, cols].bitcast(FP8X4), rhs_scale=scales[:, g, cols],
                     start=(g == 0), stop=(g == PASSES - 1),
                 )
@@ -186,48 +234,42 @@ def tile_additivemilpatchcontributionlogits_x2_kernel(
             nc.vector.scalar_tensor_tensor(
                 out=terms[:], in0=held["tanh_v", i // 2][:, i % 2, :], scalar=-0.5,
                 in1=held["gate", i // 2][:, i % 2, :], op0=ALU.mult, op1=ALU.mult,
-                accum_out=neg_e[b][:, t : t + 1],
+                accum_out=neg_e[b // 2][:, b % 2, t : t + 1],
             )
 
-        def min_local(b):
-            nc.vector.tensor_reduce(out=part_min[b][:], in_=neg_e[b][:], axis=AXIS.X, op=ALU.min)
+        def min_local(k):
+            nc.vector.tensor_reduce(out=part_min[k][:], in_=neg_e[k][:], axis=AXIS.X, op=ALU.min)
 
-        def spread_column(column):
+
+        def min_spread(k):
             bank = next_bank()
-            nc.tensor.transpose(bank[:, 0:P], column.to_broadcast([P, P]), ident[:])
-            return bank
+            for s in range(2):
+                nc.tensor.transpose(bank[:, s * P : (s + 1) * P], part_min[k][:, s : s + 1].to_broadcast([P, P]), ident[:])
+            held["min_bank", k] = bank
 
-        def min_spread(b):
-            held["min_bank", b] = spread_column(part_min[b][:])
-
-        def min_all(b):
-            bag_min = work.tile([P, 1], F32, name="bag_min")
-            nc.vector.tensor_reduce(out=bag_min[:], in_=held["min_bank", b][:, 0:P], axis=AXIS.X, op=ALU.min)
-            held["bag_min", b] = bag_min
+        def min_all(k):
+            spread = held["min_bank", k][:, 0 : 2 * P].rearrange("p (s n) -> p s n", s=2)
+            nc.vector.tensor_reduce(out=bag_min[k][:], in_=spread, axis=AXIS.X, op=ALU.min)
 
         def exponent(b):
+            k, s = divmod(b, 2)
             nc.scalar.activation(
-                out=expo[b][:], in_=neg_e[b][:], func=ACT.Exp, scale=-1.0, bias=held["bag_min", b][:],
-                accum_out=part_sum[b][:],
+                out=expo[b][:], in_=neg_e[k][:, s, :], func=ACT.Exp, scale=-1.0, bias=bag_min[k][:, s : s + 1],
+                accum_out=part_sum[k][:, s : s + 1],
             )
 
-        def sum_spread(b):
-            held["sum_bank", b] = spread_column(part_sum[b][:])
+        def mean_matmul(k):
+            bank = next_bank()
+            nc.tensor.matmul(bank[:, 0:2], lhsT=per_patch[:], rhs=part_sum[k][:], start=True, stop=True)
+            held["mean_bank", k] = bank
 
-        def sum_all(b):
-            total = work.tile([P, 1], F32, name="total")
-            nc.vector.tensor_reduce(out=total[:], in_=held["sum_bank", b][:, 0:P], axis=AXIS.X, op=ALU.add)
-            held["total", b] = total
 
-        def invert(b):
-            inverse = work.tile([P, 1], F32, name="inverse")
-            nc.vector.reciprocal(out=inverse[:], in_=held["total", b][:])
-            held["inverse", b] = inverse
+        def invert(k):
+            nc.vector.reciprocal(out=inverse[k][:], in_=held["mean_bank", k][:, 0:2])
 
         def normalise(b):
-            nc.vector.tensor_scalar(
-                out=attn[b][:], in0=expo[b][:], scalar1=held["inverse", b][:], scalar2=float(N), op0=ALU.mult, op1=ALU.mult
-            )
+            k, s = divmod(b, 2)
+            nc.scalar.activation(out=attn[b][:], in_=expo[b][:], func=ACT.Copy, scale=inverse[k][:, s : s + 1])
 
         def z_matmul(i, half):
             bank = next_bank()
@@ -245,54 +287,97 @@ def tile_additivemilpatchcontributionlogits_x2_kernel(
                     in1=b1_all[:, half, u], op0=ALU.mult, op1=ALU.add,
                 )
 
-        def p_turn(i):
+        def turn_p(i, halves):
             words = held["pre", i][:].rearrange("p g u m e -> p (g u m e)").bitcast(F32)
             bank = next_bank()
-            for g in range(PASSES):
+            for n, g in enumerate(halves):
                 for u in range(2):
-                    src, col = (g * 2 + u) * P, (u * PASSES + g) * P
+                    src, col = (g * 2 + u) * P, (u * len(halves) + n) * P
                     nc.tensor.transpose(bank[:, col : col + P], words[:, src : src + P], ident[:])
-            held["p_bank", i] = bank
+            held["p_bank", i, halves[0]] = bank
 
-        def p_relu(i):
-            grouped = work.tile([P, F], BF16, name="p_grouped", align_bytes=64)
-            dst = grouped[:].rearrange("p (q u e) -> p q u e", u=2, e=2)
-            src = held["p_bank", i][:].bitcast(BF16).rearrange("p (u q e) -> p q u e", u=2, e=2)
-            if i in RELU_ON_VECTOR:
+        def p_turn(i):
+            turn_p(i, (0, 1))
+
+        def last_turn(g):
+            turn_p(TILES - 1, (g,))
+
+        def relu_p(i, first, count, on_vector):
+            if i % 2 == 0:
+                held["p_grouped", i // 2] = work.tile([P, 2, F], BF16, name="p_grouped", align_bytes=64)
+            cols = slice(first * BANK, (first + count) * BANK)
+            dst = held["p_grouped", i // 2][:, i % 2, cols].rearrange("p (q u e) -> p q u e", u=2, e=2)
+            src = held["p_bank", i, first][:].bitcast(BF16)[:, 0 : count * BANK].rearrange("p (u q e) -> p q u e", u=2, e=2)
+            if on_vector:
                 nc.vector.tensor_scalar(out=dst, in0=src, scalar1=0.0, scalar2=None, op0=ALU.max)
             else:
                 nc.scalar.activation(out=dst, in_=src, func=ACT.Relu)
-            held["p_grouped", i] = grouped
 
-        def p_quant(i):
-            codes = work.tile([P, PASSES * P], U32, name="p_codes", align_bytes=64, bufs=8)
-            scales = work.tile([P, PASSES * P], U8, name="p_scales", align_bytes=64, bufs=8)
-            nc.vector.quantize_mx(out=codes[:].bitcast(FP8X4), scales=scales[:], in_=held["p_grouped", i][:])
-            held["p_quant", i] = (codes, scales)
+        def p_relu(i):
+            relu_p(i, 0, 2, i in RELU_ON_VECTOR)
+
+        def last_relu(g):
+            relu_p(TILES - 1, g, 1, g in LAST_RELU_ON_VECTOR)
+
+        def quant_p(j, first, count):
+            if first == 0:
+                codes = work.tile([P, 2 * PASSES * P], U32, name="p_codes", align_bytes=64, bufs=8)
+                scales = work.tile([P, 2 * PASSES * P], U8, name="p_scales", align_bytes=64, bufs=8)
+                held["p_quant", j] = (codes, scales)
+            codes, scales = held["p_quant", j]
+            cols = slice(first * P, (first + count) * P)
+            src = held["p_grouped", j][:].rearrange("p s f -> p (s f)")[:, first * BANK : (first + count) * BANK]
+            nc.vector.quantize_mx(out=codes[:, cols].bitcast(FP8X4), scales=scales[:, cols], in_=src)
+
+        def p_quant(j):
+            quant_p(j, 0, 4)
+
+        def p_quant_one(i):
+            quant_p(i // 2, 0, 2)
+
+        def last_quant(g):
+            quant_p(PAIRS - 1, 2 + g, 1)
+
+        def out_pass(out, i, g):
+            codes, scales = held["p_quant", i // 2]
+            k = slice((2 * (i % 2) + g) * P, (2 * (i % 2) + g + 1) * P)
+            nc.tensor.matmul_mx(
+                out=out, lhsT=codes[:, k].bitcast(FP8X4), lhsT_scale=scales[:, k],
+                rhs=w2_c[:, g, :].bitcast(FP8X4), rhs_scale=w2_s[:, g, :],
+                start=(g == 0), stop=(g == PASSES - 1),
+            )
 
         def out_matmul(i):
             b, t = divmod(i, PACK)
             if t == 0:
                 held["out_bank", b] = next_bank()
-            codes, scales = held["p_quant", i]
             for g in range(PASSES):
-                k = slice(g * P, (g + 1) * P)
-                nc.tensor.matmul_mx(
-                    out=held["out_bank", b][:, t * C : (t + 1) * C],
-                    lhsT=codes[:, k].bitcast(FP8X4), lhsT_scale=scales[:, k],
-                    rhs=w2_c[:, g, :].bitcast(FP8X4), rhs_scale=w2_s[:, g, :],
-                    start=(g == 0), stop=(g == PASSES - 1),
-                )
+                out_pass(held["out_bank", b][:, t * C : (t + 1) * C], i, g)
+
+        def last_matmul(g):
+            if g == 0:
+                held["last_bank"] = next_bank()
+            out_pass(held["last_bank"][:, 0:C], TILES - 1, g)
+
+        def copy_out(b, src, t0, t1):
+            if t0 == 0:
+                held["result", b] = work.tile([P, PACK * C], F32, name="result")
+            cols = slice(t0 * C, t1 * C)
+            nc.scalar.copy(out=held["result", b][:, cols], in_=src)
+            nc.sync.dma_start(out=out_0[b].rearrange("(p t) c -> p (t c)", t=PACK)[:, cols], in_=held["result", b][:, cols])
 
         def out_copy(b):
-            result = work.tile([P, PACK * C], F32, name="result")
-            nc.scalar.copy(out=result[:], in_=held["out_bank", b][:])
-            nc.sync.dma_start(out=out_0[b].rearrange("(p t) c -> p (t c)", t=PACK), in_=result[:])
-            held["result", b] = result
+            copy_out(b, held["out_bank", b][:], 0, PACK)
+
+        def out_copy_first(b):
+            copy_out(B - 1, held["out_bank", B - 1][:, 0 : (PACK - 1) * C], 0, PACK - 1)
+
+        def out_copy_last(b):
+            copy_out(B - 1, held["last_bank"][:, 0:C], PACK - 1, PACK)
 
         def out_round(b):
             grouped = work.tile([P, C, PACK], BF16, name="out_grouped", align_bytes=64)
-            if b == B - 1:
+            if b in ROUND_ON_VECTOR:
                 nc.vector.tensor_copy(out=grouped[:], in_=held["result", b][:].rearrange("p (t c) -> p c t", t=PACK))
             else:
                 nc.scalar.copy(out=grouped[:], in_=held["out_bank", b][:].rearrange("p (t c) -> p c t", t=PACK))
@@ -315,54 +400,15 @@ def tile_additivemilpatchcontributionlogits_x2_kernel(
                     out=out_2[0, 4 * q : 4 * q + 4, :].bitcast(I32), in_=out_scales[32 * q : 32 * q + 4, :].bitcast(I32)
                 )
 
-        H_ROUNDS = [range(0, 2), range(2, 6), range(6, 10), range(10, 14), range(14, 16)]
-        Z_ROUNDS = [range(0, 4), range(4, 8), range(8, 12), range(12, 14), range(14, 16)]
-        Z_FIRST = len(H_ROUNDS)
-
-        def of_round(rounds, r):
-            return rounds[r] if 0 <= r < len(rounds) else range(0)
-
-        for r in range(Z_FIRST + len(Z_ROUNDS) + 2):
-            if 0 <= r - 4 < B:
-                min_spread(r - 4)
-                min_all(r - 4)
-                exponent(r - 4)
-            if 0 <= r - 5 < B:
-                sum_spread(r - 5)
-                sum_all(r - 5)
-                invert(r - 5)
-                normalise(r - 5)
-            for i in of_round(H_ROUNDS, r):
-                h_turn(i)
-                h_copy(i)
-                h_quant(i)
-            for i in of_round(Z_ROUNDS, r - Z_FIRST - 1):
-                p_turn(i)
-                p_relu(i)
-                p_quant(i)
-            if r == 0:
-                spread_wa()
-            for j in [i // 2 for i in of_round(H_ROUNDS, r - 1) if i % 2 == 1]:
-                u_matmul(j)
-                u_tanh(j)
-                v_matmul(j)
-                v_tanh(j)
-                gate_weigh(j)
-                score(2 * j)
-                score(2 * j + 1)
-                if j % 2 == 1:
-                    min_local(j // 2)
-            if r == 1:
-                spread_b1(0)
-                spread_b1(1)
-            for i in of_round(Z_ROUNDS, r - Z_FIRST):
-                for half in range(2):
-                    z_matmul(i, half)
-                    z_affine(i, half)
-            for i in of_round(Z_ROUNDS, r - Z_FIRST - 2):
-                out_matmul(i)
-                if i % PACK == PACK - 1:
-                    out_copy(i // PACK)
-                    out_round(i // PACK)
-                    out_quant(i // PACK)
+        steps = {
+            "HT": h_turn, "HC": h_copy, "HQ": h_quant, "UU": u_matmul, "VV": v_matmul, "TU": u_tanh, "TV": v_tanh,
+            "G1": gate_weigh, "G2": score, "M4": min_local, "EA": min_spread, "MX": min_all, "EX": exponent,
+            "EB": mean_matmul, "RC": invert, "AM": normalise, "PT": p_turn, "PTh": last_turn, "PR": p_relu,
+            "PRh": last_relu, "PQ": p_quant, "PQ1": p_quant_one, "PQh": last_quant, "O": out_matmul, "Oh": last_matmul,
+            "OC": out_copy, "OCa": out_copy_first, "OCb": out_copy_last, "OB": out_round, "OQ": out_quant,
+            "BC": spread_matmul, "BCs": spread_copy,
+            "Z": lambda n: z_matmul(n // 2, n % 2), "ZE": lambda n: z_affine(n // 2, n % 2),
+        }
+        for name, index in ORDER:
+            steps[name](index)
         store_scales()

@@ -24,40 +24,42 @@ TILES = B * PACK
 PAIRS = TILES // 2
 ROTATING_BANKS = 8
 RELU_ON_VECTOR = ()
-LAST_RELU_ON_VECTOR = ()
-H_COPY_ON_VECTOR = (2,)
-ROUND_ON_VECTOR = (1, 3, 2,)
-GATE_ON_GPSIMD = ()
+LAST_RELU_ON_VECTOR = (0,)
+H_COPY_ON_VECTOR = (0, 4, 2, 5,)
+ROUND_ON_VECTOR = (3, 2, 1,)
+GATE_ON_GPSIMD = (7, 4, 5, 6, 0,)
+STEPPED_TURN = (3, 7, 8, 12, 13, 14, 15,)
+WARM_MATMULS = 4
 ORDER = [
-    ("HT", 0), ("HT", 1), ("HC", 0), ("HT", 2), ("HC", 1), ("HT", 3), ("HQ", 0), ("BC", 0), ("HC", 2),
-    ("HC", 3), ("UU", 0), ("BCs", 0), ("VV", 0), ("TU", 0), ("HQ", 1), ("HT", 4), ("TV", 0), ("G1", 0),
-    ("HT", 5), ("HC", 4), ("HT", 6), ("G2", 0), ("HC", 5), ("HT", 7), ("G2", 1), ("HC", 6), ("BC", 1),
-    ("HQ", 2), ("UU", 1), ("HC", 7), ("BCs", 1), ("BC", 2), ("VV", 1), ("TU", 1), ("HQ", 3), ("UU", 2),
-    ("G1", 1), ("TV", 1), ("UU", 3), ("BCs", 2), ("TU", 2), ("HT", 8), ("G2", 2), ("TU", 3), ("HT", 9),
-    ("G2", 3), ("HC", 8), ("G1", 2), ("VV", 2), ("HC", 9), ("VV", 3), ("G1", 3), ("TV", 2), ("HQ", 4),
-    ("HT", 10), ("TV", 3), ("HT", 11), ("G2", 4), ("HC", 10), ("G2", 5), ("UU", 4), ("G2", 6), ("HC", 11),
-    ("VV", 4), ("G2", 7), ("TU", 4), ("HT", 12), ("HQ", 5), ("TV", 4), ("HT", 13), ("M4", 0), ("G1", 4),
-    ("HC", 12), ("EA", 0), ("UU", 5), ("HC", 13), ("MX", 0), ("G2", 8), ("HT", 14), ("EX", 0), ("EX", 1),
-    ("G2", 9), ("TU", 5), ("EB", 0), ("HQ", 6), ("Z", 0), ("HC", 14), ("VV", 5), ("RC", 0), ("G1", 5),
-    ("AM", 0), ("AM", 1), ("Z", 1), ("ZE", 0), ("TV", 5), ("HT", 15), ("ZE", 1), ("UU", 6), ("HC", 15),
-    ("G2", 10), ("Z", 2), ("G2", 11), ("TU", 6), ("Z", 3), ("HQ", 7), ("PT", 0), ("ZE", 2), ("Z", 4),
-    ("PR", 0), ("ZE", 3), ("Z", 5), ("ZE", 4), ("Z", 6), ("Z", 7), ("ZE", 5), ("VV", 6), ("ZE", 6), ("Z", 8),
-    ("TV", 6), ("ZE", 7), ("UU", 7), ("ZE", 8), ("VV", 7), ("TU", 7), ("G1", 6), ("PT", 1), ("TV", 7),
-    ("PT", 2), ("G1", 7), ("Z", 9), ("PR", 1), ("G2", 12), ("PT", 3), ("G2", 13), ("Z", 10), ("PR", 2),
-    ("ZE", 9), ("ZE", 10), ("PT", 4), ("PR", 3), ("Z", 11), ("G2", 14), ("G2", 15), ("Z", 12), ("PR", 4),
-    ("ZE", 11), ("Z", 13), ("M4", 1), ("ZE", 12), ("EA", 1), ("Z", 14), ("ZE", 13), ("Z", 15), ("MX", 1),
-    ("Z", 16), ("ZE", 14), ("EX", 2), ("EX", 3), ("PT", 5), ("ZE", 15), ("PT", 6), ("PR", 5), ("EB", 1),
-    ("PQ", 0), ("Z", 17), ("RC", 1), ("Z", 18), ("PQ", 1), ("AM", 2), ("AM", 3), ("PR", 6), ("PT", 7),
-    ("ZE", 16), ("Z", 19), ("ZE", 17), ("PR", 7), ("O", 0), ("O", 1), ("O", 2), ("ZE", 18), ("Z", 20),
-    ("Z", 21), ("ZE", 19), ("Z", 22), ("ZE", 20), ("O", 3), ("Z", 23), ("ZE", 21), ("OC", 0), ("PT", 8),
-    ("ZE", 22), ("PT", 9), ("OB", 0), ("PT", 10), ("ZE", 23), ("PR", 8), ("Z", 24), ("PQ", 2), ("Z", 25),
-    ("PR", 9), ("ZE", 24), ("Z", 26), ("Z", 27), ("ZE", 25), ("PR", 10), ("PT", 11), ("ZE", 26), ("Z", 28),
-    ("ZE", 27), ("PR", 11), ("PT", 12), ("ZE", 28), ("Z", 29), ("PR", 12), ("Z", 30), ("PQ", 3), ("PT", 13),
-    ("ZE", 29), ("O", 4), ("PR", 13), ("ZE", 30), ("PT", 14), ("O", 5), ("PQ", 4), ("O", 6), ("Z", 31),
-    ("PR", 14), ("PQ", 5), ("PTh", 0), ("O", 7), ("ZE", 31), ("O", 8), ("PRh", 0), ("PQ", 6), ("OC", 1),
-    ("PTh", 1), ("O", 9), ("O", 10), ("PQ1", 14), ("PRh", 1), ("O", 11), ("O", 12), ("PQh", 0), ("O", 13),
-    ("OB", 1), ("O", 14), ("OC", 2), ("Oh", 0), ("PQh", 1), ("OQ", 0), ("OCa", 0), ("Oh", 1), ("OQ", 1),
-    ("OB", 2), ("OCb", 0), ("OB", 3), ("OQ", 2), ("OQ", 3),
+    ("HT", 0), ("HT", 1), ("HC", 0), ("BC", 0), ("HC", 1), ("HT", 2), ("HT", 3), ("HQ", 0), ("BCs", 0),
+    ("HC", 3), ("UU", 0), ("HC", 2), ("VV", 0), ("TU", 0), ("HQ", 1), ("HT", 4), ("TV", 0), ("HT", 5),
+    ("HC", 4), ("G1", 0), ("HT", 6), ("HC", 5), ("UU", 1), ("HC", 6), ("VV", 1), ("G2", 0), ("TU", 1),
+    ("HT", 7), ("G2", 1), ("TV", 1), ("HQ", 2), ("HT", 8), ("HC", 7), ("HT", 9), ("G1", 1), ("HC", 8),
+    ("UU", 2), ("HQ", 3), ("HC", 9), ("VV", 2), ("G2", 2), ("VV", 3), ("HQ", 4), ("TV", 2), ("UU", 3),
+    ("G2", 3), ("TV", 3), ("G1", 2), ("HT", 10), ("TU", 2), ("G1", 3), ("HT", 11), ("TU", 3), ("HT", 12),
+    ("G2", 4), ("HC", 10), ("G2", 5), ("VV", 4), ("G2", 6), ("HC", 11), ("BC", 1), ("G2", 7), ("UU", 4),
+    ("TV", 4), ("HQ", 5), ("BC", 2), ("HC", 12), ("HT", 13), ("G1", 4), ("M4", 0), ("BCs", 1), ("TU", 4),
+    ("EA", 0), ("Z", 0), ("MX", 0), ("HC", 13), ("BCs", 2), ("UU", 5), ("EX", 0), ("EX", 1), ("VV", 5),
+    ("HQ", 6), ("EB", 0), ("G2", 8), ("Z", 1), ("TV", 5), ("RC", 0), ("G2", 9), ("Z", 2), ("AM", 0),
+    ("AM", 1), ("G1", 5), ("TU", 5), ("ZE", 0), ("Z", 3), ("Z", 4), ("ZE", 1), ("VV", 6), ("G2", 10),
+    ("Z", 5), ("ZE", 2), ("TV", 6), ("Z", 6), ("ZE", 3), ("G1", 6), ("PT", 0), ("ZE", 4), ("HT", 14),
+    ("PR", 0), ("HT", 15), ("ZE", 5), ("PT", 1), ("ZE", 6), ("HC", 14), ("Z", 7), ("G2", 11), ("HC", 15),
+    ("UU", 6), ("ZE", 7), ("Z", 8), ("PR", 1), ("HQ", 7), ("Z", 9), ("ZE", 8), ("Z", 10), ("VV", 7),
+    ("ZE", 9), ("Z", 11), ("ZE", 10), ("TV", 7), ("Z", 12), ("TU", 6), ("ZE", 11), ("G1", 7), ("UU", 7),
+    ("ZE", 12), ("PT", 2), ("TU", 7), ("PT", 3), ("G2", 12), ("PR", 2), ("PT", 4), ("G2", 13), ("Z", 13),
+    ("G2", 14), ("Z", 14), ("PR", 3), ("G2", 15), ("Z", 15), ("PQ", 0), ("PR", 4), ("M4", 1), ("PT", 5),
+    ("ZE", 13), ("EA", 1), ("Z", 16), ("MX", 1), ("ZE", 14), ("Z", 17), ("EX", 2), ("EX", 3), ("PR", 5),
+    ("Z", 18), ("ZE", 15), ("EB", 1), ("PQ", 1), ("Z", 19), ("RC", 1), ("PQ", 2), ("PT", 6), ("AM", 2),
+    ("PT", 7), ("PR", 6), ("ZE", 16), ("Z", 20), ("ZE", 17), ("Z", 21), ("AM", 3), ("ZE", 18), ("PR", 7),
+    ("O", 0), ("O", 1), ("O", 2), ("O", 3), ("ZE", 19), ("Z", 22), ("OC", 0), ("ZE", 20), ("Z", 23),
+    ("Z", 24), ("OB", 0), ("ZE", 21), ("PT", 8), ("ZE", 22), ("PT", 9), ("PR", 8), ("ZE", 23), ("PT", 10),
+    ("Z", 25), ("ZE", 24), ("Z", 26), ("PR", 9), ("ZE", 25), ("Z", 27), ("ZE", 26), ("Z", 28), ("PR", 10),
+    ("ZE", 27), ("PT", 11), ("PT", 12), ("ZE", 28), ("PR", 11), ("PT", 13), ("PQ", 3), ("Z", 29), ("PQ", 4),
+    ("PR", 12), ("Z", 30), ("ZE", 29), ("O", 4), ("O", 5), ("PR", 13), ("O", 6), ("ZE", 30), ("Z", 31),
+    ("PQ", 5), ("O", 7), ("PT", 14), ("OC", 1), ("ZE", 31), ("PTh", 0), ("PR", 14), ("O", 8), ("PQ", 6),
+    ("PTh", 1), ("OQ", 0), ("O", 9), ("O", 10), ("PRh", 0), ("O", 11), ("PRh", 1), ("O", 12), ("PQ1", 14),
+    ("O", 13), ("PQh", 0), ("OC", 2), ("O", 14), ("PQh", 1), ("Oh", 0), ("OB", 1), ("Oh", 1), ("OCa", 0),
+    ("OB", 2), ("OCb", 0), ("OQ", 1), ("OB", 3), ("OQ", 2), ("OQ", 3),
 ]
 
 
@@ -70,7 +72,7 @@ def tile_additivemilpatchcontributionlogits_x2_kernel(
         keep = ctx.enter_context(tc.tile_pool(name="keep", bufs=1))
         work = ctx.enter_context(tc.tile_pool(name="work", bufs=4))
         psum = ctx.enter_context(tc.psum_pool(name="psum", bufs=1))
-        ctx.enter_context(tc.manual_schedule(engines={mybir.EngineType.PE, mybir.EngineType.SP, mybir.EngineType.Activation, mybir.EngineType.DVE}))
+        ctx.enter_context(tc.manual_schedule(engines={mybir.EngineType.PE, mybir.EngineType.SP, mybir.EngineType.Activation, mybir.EngineType.DVE, mybir.EngineType.Pool}))
 
         banks_taken = []
 
@@ -101,12 +103,15 @@ def tile_additivemilpatchcontributionlogits_x2_kernel(
         def load_h(b, t0, t1):
             nc.sync.dma_start(out=h_raw[b][:, t0:t1, :], in_=h[b].rearrange("(p t) d -> p t d", t=PACK)[:, t0:t1, :])
 
+        warm = keep.tile([P, BANK], BF16)
+        nc.gpsimd.memset(warm[:], 0.0)
+        warm_bank = next_bank()
+        for n in range(WARM_MATMULS):
+            nc.tensor.matmul(warm_bank[:], lhsT=warm[:, 0:P], rhs=warm[:], start=True, stop=True)
         ident = keep.tile([P, P], F32)
         make_identity(nc, ident[:])
         wu_c, wu_s = weight_tiles("wu", A)
         wv_c, wv_s = weight_tiles("wv", A)
-        zeros = keep.tile([P, P], BF16)
-        nc.vector.memset(zeros[:], 0.0)
         wa_row = keep.tile([P, A], BF16)
         nc.vector.memset(wa_row[:], 0.0)
         b1_row = keep.tile([P, F], BF16)
@@ -115,7 +120,7 @@ def tile_additivemilpatchcontributionlogits_x2_kernel(
         w2_c, w2_s = weight_tiles("w2", C)
 
         ones = keep.tile([P, P], BF16)
-        nc.scalar.activation(out=ones[:], in_=zeros[:], func=ACT.Exp)
+        nc.scalar.activation(out=ones[:], in_=warm[:, 0:P], func=ACT.Exp)
         per_patch = keep.tile([P, P], F32)
         nc.gpsimd.memset(per_patch[:], 1.0 / N)
         nc.gpsimd.dma_start(out=wa_row[0:1, :], in_=wa.unsqueeze(0))
@@ -136,7 +141,7 @@ def tile_additivemilpatchcontributionlogits_x2_kernel(
         load_codes(w2_c, w2_words, 0, 2)
 
         wa_all = keep.tile([P, A], F32)
-        b1_all = keep.tile([P, PASSES, 2, P, 2], F32)
+        b1_all = keep.tile([P, PASSES, BANK], F32)
         h_codes = [keep.tile([P, 2, PASSES * P], U32, name="h_codes%d" % j, align_bytes=64) for j in range(PAIRS)]
         h_scales = [keep.tile([P, 2, PASSES * P], U8, name="h_scales%d" % j, align_bytes=64) for j in range(PAIRS)]
         neg_e = [keep.tile([P, 2, PACK], F32, name="neg_e%d" % k) for k in range(B // 2)]
@@ -159,9 +164,9 @@ def tile_additivemilpatchcontributionlogits_x2_kernel(
         def spread_copy(k):
             bank = held["row_bank", k]
             if k == 0:
-                nc.vector.tensor_copy(out=wa_all[:], in_=bank[:, 0:A])
+                nc.vector.tensor_scalar(out=wa_all[:], in0=bank[:, 0:A], scalar1=-0.5, scalar2=None, op0=ALU.mult)
             else:
-                nc.vector.tensor_copy(out=b1_all[:, k - 1], in_=bank[:].rearrange("p (m u e) -> p u m e", u=2, e=2))
+                nc.vector.tensor_copy(out=b1_all[:, k - 1, :], in_=bank[:])
 
         def h_turn(i):
             words = h_raw[i // PACK][:, i % PACK, :].bitcast(F32)
@@ -173,7 +178,7 @@ def tile_additivemilpatchcontributionlogits_x2_kernel(
             held["h_bank", i] = bank
 
         def h_copy(i):
-            if i % 2 == 0:
+            if ("h_grouped", i // 2) not in held:
                 held["h_grouped", i // 2] = work.tile([P, 2, D], BF16, name="h_grouped", align_bytes=64)
             dst = held["h_grouped", i // 2][:, i % 2, :].bitcast(F32).rearrange("p (q u) -> p q u", u=2)
             src = held["h_bank", i][:].rearrange("p (u q) -> p q u", u=2)
@@ -222,9 +227,9 @@ def tile_additivemilpatchcontributionlogits_x2_kernel(
 
         def gate_weigh(j):
             gate = work.tile([P, 2, A], F32, name="gate")
-            nc.vector.scalar_tensor_tensor(
-                out=gate[:], in0=held["tanh_u", j][:], scalar=1.0,
-                in1=wa_all[:].unsqueeze(1).to_broadcast([P, 2, A]), op0=ALU.add, op1=ALU.mult,
+            engine = nc.gpsimd if j in GATE_ON_GPSIMD else nc.vector
+            engine.tensor_tensor(
+                out=gate[:], in0=held["tanh_v", j][:], in1=wa_all[:].unsqueeze(1).to_broadcast([P, 2, A]), op=ALU.mult
             )
             held["gate", j] = gate
 
@@ -232,8 +237,8 @@ def tile_additivemilpatchcontributionlogits_x2_kernel(
             terms = work.tile([P, A], F32, name="terms")
             b, t = divmod(i, PACK)
             nc.vector.scalar_tensor_tensor(
-                out=terms[:], in0=held["tanh_v", i // 2][:, i % 2, :], scalar=-0.5,
-                in1=held["gate", i // 2][:, i % 2, :], op0=ALU.mult, op1=ALU.mult,
+                out=terms[:], in0=held["tanh_u", i // 2][:, i % 2, :], scalar=1.0,
+                in1=held["gate", i // 2][:, i % 2, :], op0=ALU.add, op1=ALU.mult,
                 accum_out=neg_e[b // 2][:, b % 2, t : t + 1],
             )
 
@@ -278,22 +283,31 @@ def tile_additivemilpatchcontributionlogits_x2_kernel(
 
         def z_affine(i, half):
             if half == 0:
-                held["pre", i] = work.tile([P, PASSES, 2, P, 2], BF16, name="pre", bufs=8)
+                held["pre", i] = work.tile([P, PASSES, BANK], BF16, name="pre", bufs=8)
             b, t = divmod(i, PACK)
-            z = held["z_bank", i, half][:].rearrange("p (m u e) -> p u m e", u=2, e=2)
-            for u in range(2):
+            z, bias, pre = held["z_bank", i, half][:], b1_all[:, half, :], held["pre", i][:, half, :]
+            if i in STEPPED_TURN:
+                parts = [(z, bias, pre)]
+            else:
+                z, bias = [x.rearrange("p (m u e) -> p u m e", u=2, e=2) for x in (z, bias)]
+                pre = pre.rearrange("p (u m e) -> p u m e", u=2, e=2)
+                parts = [(z[:, u], bias[:, u], pre[:, u]) for u in range(2)]
+            for z_part, bias_part, pre_part in parts:
                 nc.vector.scalar_tensor_tensor(
-                    out=held["pre", i][:, half, u], in0=z[:, u], scalar=attn[b][:, t : t + 1],
-                    in1=b1_all[:, half, u], op0=ALU.mult, op1=ALU.add,
+                    out=pre_part, in0=z_part, scalar=attn[b][:, t : t + 1], in1=bias_part, op0=ALU.mult, op1=ALU.add
                 )
 
         def turn_p(i, halves):
-            words = held["pre", i][:].rearrange("p g u m e -> p (g u m e)").bitcast(F32)
+            words = held["pre", i][:].rearrange("p g f -> p (g f)").bitcast(F32)
             bank = next_bank()
             for n, g in enumerate(halves):
                 for u in range(2):
-                    src, col = (g * 2 + u) * P, (u * len(halves) + n) * P
-                    nc.tensor.transpose(bank[:, col : col + P], words[:, src : src + P], ident[:])
+                    col = (u * len(halves) + n) * P
+                    if i in STEPPED_TURN:
+                        src = words[:, 256 * g + u : 256 * (g + 1) : 2]
+                    else:
+                        src = words[:, (g * 2 + u) * P : (g * 2 + u + 1) * P]
+                    nc.tensor.transpose(bank[:, col : col + P], src, ident[:])
             held["p_bank", i, halves[0]] = bank
 
         def p_turn(i):
@@ -303,7 +317,7 @@ def tile_additivemilpatchcontributionlogits_x2_kernel(
             turn_p(TILES - 1, (g,))
 
         def relu_p(i, first, count, on_vector):
-            if i % 2 == 0:
+            if ("p_grouped", i // 2) not in held:
                 held["p_grouped", i // 2] = work.tile([P, 2, F], BF16, name="p_grouped", align_bytes=64)
             cols = slice(first * BANK, (first + count) * BANK)
             dst = held["p_grouped", i // 2][:, i % 2, cols].rearrange("p (q u e) -> p q u e", u=2, e=2)
@@ -360,7 +374,7 @@ def tile_additivemilpatchcontributionlogits_x2_kernel(
             out_pass(held["last_bank"][:, 0:C], TILES - 1, g)
 
         def copy_out(b, src, t0, t1):
-            if t0 == 0:
+            if ("result", b) not in held:
                 held["result", b] = work.tile([P, PACK * C], F32, name="result")
             cols = slice(t0 * C, t1 * C)
             nc.scalar.copy(out=held["result", b][:, cols], in_=src)

@@ -24,42 +24,42 @@ TILES = B * PACK
 PAIRS = TILES // 2
 ROTATING_BANKS = 8
 RELU_ON_VECTOR = ()
-LAST_RELU_ON_VECTOR = (0,)
-H_COPY_ON_VECTOR = (0, 4, 2, 5,)
-ROUND_ON_VECTOR = (3, 2, 1,)
-GATE_ON_GPSIMD = (7, 4, 5, 6, 0,)
-STEPPED_TURN = (3, 7, 8, 12, 13, 14, 15,)
+LAST_RELU_ON_VECTOR = (0, 1,)
+H_COPY_ON_VECTOR = (9, 5, 2,)
+ROUND_ON_VECTOR = (3, 2,)
+GATE_ON_GPSIMD = (7, 5, 6,)
+STEPPED_TURN = (0, 2, 3, 5, 9, 10, 12, 14, 15,)
 WARM_MATMULS = 4
 ORDER = [
-    ("HT", 0), ("HT", 1), ("HC", 0), ("BC", 0), ("HC", 1), ("HT", 2), ("HT", 3), ("HQ", 0), ("BCs", 0),
-    ("HC", 3), ("UU", 0), ("HC", 2), ("VV", 0), ("TU", 0), ("HQ", 1), ("HT", 4), ("TV", 0), ("HT", 5),
-    ("HC", 4), ("G1", 0), ("HT", 6), ("HC", 5), ("UU", 1), ("HC", 6), ("VV", 1), ("G2", 0), ("TU", 1),
-    ("HT", 7), ("G2", 1), ("TV", 1), ("HQ", 2), ("HT", 8), ("HC", 7), ("HT", 9), ("G1", 1), ("HC", 8),
-    ("UU", 2), ("HQ", 3), ("HC", 9), ("VV", 2), ("G2", 2), ("VV", 3), ("HQ", 4), ("TV", 2), ("UU", 3),
-    ("G2", 3), ("TV", 3), ("G1", 2), ("HT", 10), ("TU", 2), ("G1", 3), ("HT", 11), ("TU", 3), ("HT", 12),
-    ("G2", 4), ("HC", 10), ("G2", 5), ("VV", 4), ("G2", 6), ("HC", 11), ("BC", 1), ("G2", 7), ("UU", 4),
-    ("TV", 4), ("HQ", 5), ("BC", 2), ("HC", 12), ("HT", 13), ("G1", 4), ("M4", 0), ("BCs", 1), ("TU", 4),
-    ("EA", 0), ("Z", 0), ("MX", 0), ("HC", 13), ("BCs", 2), ("UU", 5), ("EX", 0), ("EX", 1), ("VV", 5),
-    ("HQ", 6), ("EB", 0), ("G2", 8), ("Z", 1), ("TV", 5), ("RC", 0), ("G2", 9), ("Z", 2), ("AM", 0),
-    ("AM", 1), ("G1", 5), ("TU", 5), ("ZE", 0), ("Z", 3), ("Z", 4), ("ZE", 1), ("VV", 6), ("G2", 10),
-    ("Z", 5), ("ZE", 2), ("TV", 6), ("Z", 6), ("ZE", 3), ("G1", 6), ("PT", 0), ("ZE", 4), ("HT", 14),
-    ("PR", 0), ("HT", 15), ("ZE", 5), ("PT", 1), ("ZE", 6), ("HC", 14), ("Z", 7), ("G2", 11), ("HC", 15),
-    ("UU", 6), ("ZE", 7), ("Z", 8), ("PR", 1), ("HQ", 7), ("Z", 9), ("ZE", 8), ("Z", 10), ("VV", 7),
-    ("ZE", 9), ("Z", 11), ("ZE", 10), ("TV", 7), ("Z", 12), ("TU", 6), ("ZE", 11), ("G1", 7), ("UU", 7),
-    ("ZE", 12), ("PT", 2), ("TU", 7), ("PT", 3), ("G2", 12), ("PR", 2), ("PT", 4), ("G2", 13), ("Z", 13),
-    ("G2", 14), ("Z", 14), ("PR", 3), ("G2", 15), ("Z", 15), ("PQ", 0), ("PR", 4), ("M4", 1), ("PT", 5),
-    ("ZE", 13), ("EA", 1), ("Z", 16), ("MX", 1), ("ZE", 14), ("Z", 17), ("EX", 2), ("EX", 3), ("PR", 5),
-    ("Z", 18), ("ZE", 15), ("EB", 1), ("PQ", 1), ("Z", 19), ("RC", 1), ("PQ", 2), ("PT", 6), ("AM", 2),
-    ("PT", 7), ("PR", 6), ("ZE", 16), ("Z", 20), ("ZE", 17), ("Z", 21), ("AM", 3), ("ZE", 18), ("PR", 7),
-    ("O", 0), ("O", 1), ("O", 2), ("O", 3), ("ZE", 19), ("Z", 22), ("OC", 0), ("ZE", 20), ("Z", 23),
-    ("Z", 24), ("OB", 0), ("ZE", 21), ("PT", 8), ("ZE", 22), ("PT", 9), ("PR", 8), ("ZE", 23), ("PT", 10),
-    ("Z", 25), ("ZE", 24), ("Z", 26), ("PR", 9), ("ZE", 25), ("Z", 27), ("ZE", 26), ("Z", 28), ("PR", 10),
-    ("ZE", 27), ("PT", 11), ("PT", 12), ("ZE", 28), ("PR", 11), ("PT", 13), ("PQ", 3), ("Z", 29), ("PQ", 4),
-    ("PR", 12), ("Z", 30), ("ZE", 29), ("O", 4), ("O", 5), ("PR", 13), ("O", 6), ("ZE", 30), ("Z", 31),
-    ("PQ", 5), ("O", 7), ("PT", 14), ("OC", 1), ("ZE", 31), ("PTh", 0), ("PR", 14), ("O", 8), ("PQ", 6),
-    ("PTh", 1), ("OQ", 0), ("O", 9), ("O", 10), ("PRh", 0), ("O", 11), ("PRh", 1), ("O", 12), ("PQ1", 14),
-    ("O", 13), ("PQh", 0), ("OC", 2), ("O", 14), ("PQh", 1), ("Oh", 0), ("OB", 1), ("Oh", 1), ("OCa", 0),
-    ("OB", 2), ("OCb", 0), ("OQ", 1), ("OB", 3), ("OQ", 2), ("OQ", 3),
+    ("HT", 0), ("HT", 1), ("HC", 0), ("W", 0), ("HC", 1), ("HT", 2), ("HQ", 0), ("HT", 3), ("HC", 2),
+    ("BC", 0), ("VV", 0), ("HC", 3), ("BCs", 0), ("HT", 4), ("HQ", 1), ("TV", 0), ("HT", 5), ("HC", 4),
+    ("G1", 0), ("HT", 6), ("HT", 7), ("HC", 5), ("HC", 6), ("VV", 1), ("HQ", 2), ("HC", 7), ("UU", 0),
+    ("TV", 1), ("HQ", 3), ("VV", 2), ("TU", 0), ("G1", 1), ("HT", 8), ("TV", 2), ("HT", 9), ("G2", 0),
+    ("HC", 8), ("G2", 1), ("HT", 10), ("HC", 9), ("VV", 3), ("HC", 10), ("G1", 2), ("UU", 1), ("TV", 3),
+    ("HQ", 4), ("UU", 2), ("TU", 1), ("G1", 3), ("VV", 4), ("TU", 2), ("G2", 2), ("UU", 3), ("G2", 3),
+    ("UU", 4), ("G2", 4), ("TU", 3), ("HT", 11), ("G2", 5), ("TV", 4), ("HT", 12), ("G2", 6), ("HC", 11),
+    ("HT", 13), ("G2", 7), ("TU", 4), ("HT", 14), ("M4", 0), ("G1", 4), ("EA", 0), ("HC", 12), ("HT", 15),
+    ("HQ", 5), ("HC", 13), ("Z", 0), ("MX", 0), ("HC", 14), ("G2", 8), ("VV", 5), ("EX", 0), ("G2", 9),
+    ("Z", 1), ("EX", 1), ("HC", 15), ("HQ", 6), ("EB", 0), ("Z", 2), ("TV", 5), ("RC", 0), ("HQ", 7),
+    ("UU", 5), ("AM", 0), ("Z", 3), ("G1", 5), ("ZE", 0), ("TU", 5), ("VV", 6), ("ZE", 1), ("Z", 4),
+    ("ZE", 2), ("TV", 6), ("UU", 6), ("G2", 10), ("VV", 7), ("G2", 11), ("Z", 5), ("G1", 6), ("ZE", 3),
+    ("TV", 7), ("Z", 6), ("ZE", 4), ("TU", 6), ("Z", 7), ("ZE", 5), ("AM", 1), ("Z", 8), ("G1", 7), ("ZE", 6),
+    ("UU", 7), ("ZE", 7), ("Z", 9), ("TU", 7), ("Z", 10), ("ZE", 8), ("PT", 0), ("ZE", 9), ("PT", 1),
+    ("G2", 12), ("PT", 2), ("PR", 0), ("G2", 13), ("PT", 3), ("G2", 14), ("PR", 1), ("Z", 11), ("G2", 15),
+    ("Z", 12), ("ZE", 10), ("PR", 2), ("Z", 13), ("ZE", 11), ("Z", 14), ("M4", 1), ("ZE", 12), ("PR", 3),
+    ("PT", 4), ("EA", 1), ("ZE", 13), ("PT", 5), ("PR", 4), ("MX", 1), ("PT", 6), ("PQ", 0), ("Z", 15),
+    ("ZE", 14), ("EX", 2), ("Z", 16), ("EX", 3), ("PR", 5), ("PQ", 1), ("EB", 1), ("Z", 17), ("RC", 1),
+    ("ZE", 15), ("Z", 18), ("AM", 2), ("PR", 6), ("Z", 19), ("PQ", 2), ("Z", 20), ("ZE", 16), ("AM", 3),
+    ("Z", 21), ("ZE", 17), ("Z", 22), ("ZE", 18), ("PT", 7), ("PT", 8), ("ZE", 19), ("PR", 7), ("O", 0),
+    ("Z", 23), ("ZE", 20), ("O", 1), ("O", 2), ("ZE", 21), ("PR", 8), ("Z", 24), ("ZE", 22), ("O", 3),
+    ("Z", 25), ("OC", 0), ("ZE", 23), ("PT", 9), ("PT", 10), ("ZE", 24), ("OB", 0), ("PT", 11), ("PQ", 3),
+    ("PR", 9), ("Z", 26), ("ZE", 25), ("Z", 27), ("PR", 10), ("ZE", 26), ("Z", 28), ("ZE", 27), ("Z", 29),
+    ("PR", 11), ("ZE", 28), ("PT", 12), ("PT", 13), ("PQ", 4), ("PR", 12), ("O", 4), ("Z", 30), ("ZE", 29),
+    ("O", 5), ("Z", 31), ("PQ", 5), ("PR", 13), ("O", 6), ("ZE", 30), ("O", 7), ("PT", 14), ("OC", 1),
+    ("ZE", 31), ("PTh", 0), ("PR", 14), ("PQ", 6), ("PTh", 1), ("O", 8), ("PRh", 0), ("O", 9), ("O", 10),
+    ("PRh", 1), ("O", 11), ("OB", 1), ("O", 12), ("PQ1", 14), ("O", 13), ("PQh", 0), ("OC", 2), ("O", 14),
+    ("PQh", 1), ("Oh", 0), ("OQ", 0), ("Oh", 1), ("OCa", 0), ("OB", 2), ("OCb", 0), ("OQ", 1), ("OB", 3),
+    ("OQ", 2), ("OQ", 3),
 ]
 
 
@@ -110,12 +110,10 @@ def tile_additivemilpatchcontributionlogits_x2_kernel(
             nc.tensor.matmul(warm_bank[:], lhsT=warm[:, 0:P], rhs=warm[:], start=True, stop=True)
         ident = keep.tile([P, P], F32)
         make_identity(nc, ident[:])
-        wu_c, wu_s = weight_tiles("wu", A)
         wv_c, wv_s = weight_tiles("wv", A)
+        wu_c, wu_s = weight_tiles("wu", A)
         wa_row = keep.tile([P, A], BF16)
         nc.vector.memset(wa_row[:], 0.0)
-        b1_row = keep.tile([P, F], BF16)
-        nc.vector.memset(b1_row[:], 0.0)
         w1_c, w1_s = weight_tiles("w1", F)
         w2_c, w2_s = weight_tiles("w2", C)
 
@@ -124,24 +122,26 @@ def tile_additivemilpatchcontributionlogits_x2_kernel(
         per_patch = keep.tile([P, P], F32)
         nc.gpsimd.memset(per_patch[:], 1.0 / N)
         nc.gpsimd.dma_start(out=wa_row[0:1, :], in_=wa.unsqueeze(0))
-        nc.gpsimd.dma_start(out=b1_row[0:1, :], in_=b1.unsqueeze(0))
         load_h(0, 0, 1)
         load_h(0, 1, 2)
         load_h(0, 2, 4)
-        load_scales(nc.sync, wu_s, wu_scales)
-        load_codes(wu_c, wu_words, 0, 2)
         load_scales(nc.sync, wv_s, wv_scales)
         load_codes(wv_c, wv_words, 0, 2)
-        for j in range(2, PAIRS):
+        load_h(1, 0, 2)
+        load_h(1, 2, 4)
+        load_scales(nc.sync, wu_s, wu_scales)
+        load_codes(wu_c, wu_words, 0, 2)
+        for j in range(4, PAIRS):
             load_h(j // 2, 2 * (j % 2), 2 * (j % 2) + 2)
         load_scales(nc.sync, w1_s, w1_scales)
-        load_scales(nc.sync, w2_s, w2_scales)
         load_codes(w1_c, w1_words, 0, 1)
         load_codes(w1_c, w1_words, 1, 2)
+        b1_all = keep.tile([P, PASSES, BANK], BF16)
+        nc.sync.dma_start(out=b1_all[:].rearrange("p g f -> p (g f)"), in_=b1.partition_broadcast(P))
+        load_scales(nc.sync, w2_s, w2_scales)
         load_codes(w2_c, w2_words, 0, 2)
 
         wa_all = keep.tile([P, A], F32)
-        b1_all = keep.tile([P, PASSES, BANK], F32)
         h_codes = [keep.tile([P, 2, PASSES * P], U32, name="h_codes%d" % j, align_bytes=64) for j in range(PAIRS)]
         h_scales = [keep.tile([P, 2, PASSES * P], U8, name="h_scales%d" % j, align_bytes=64) for j in range(PAIRS)]
         neg_e = [keep.tile([P, 2, PACK], F32, name="neg_e%d" % k) for k in range(B // 2)]
@@ -157,16 +157,15 @@ def tile_additivemilpatchcontributionlogits_x2_kernel(
 
         def spread_matmul(k):
             bank = next_bank()
-            row = wa_row[:] if k == 0 else b1_row[:, (k - 1) * BANK : k * BANK]
-            nc.tensor.matmul(bank[:, 0 : row.shape[1]], lhsT=ones[:], rhs=row, start=True, stop=True)
+            nc.tensor.matmul(bank[:, 0:A], lhsT=ones[:], rhs=wa_row[:], start=True, stop=True)
             held["row_bank", k] = bank
 
+        def keep_warm(k):
+            for n in range(2):
+                nc.tensor.matmul(warm_bank[:], lhsT=warm[:, 0:P], rhs=warm[:], start=True, stop=True)
+
         def spread_copy(k):
-            bank = held["row_bank", k]
-            if k == 0:
-                nc.vector.tensor_scalar(out=wa_all[:], in0=bank[:, 0:A], scalar1=-0.5, scalar2=None, op0=ALU.mult)
-            else:
-                nc.vector.tensor_copy(out=b1_all[:, k - 1, :], in_=bank[:])
+            nc.vector.tensor_scalar(out=wa_all[:], in0=held["row_bank", k][:, 0:A], scalar1=-0.5, scalar2=None, op0=ALU.mult)
 
         def h_turn(i):
             words = h_raw[i // PACK][:, i % PACK, :].bitcast(F32)
@@ -420,7 +419,7 @@ def tile_additivemilpatchcontributionlogits_x2_kernel(
             "EB": mean_matmul, "RC": invert, "AM": normalise, "PT": p_turn, "PTh": last_turn, "PR": p_relu,
             "PRh": last_relu, "PQ": p_quant, "PQ1": p_quant_one, "PQh": last_quant, "O": out_matmul, "Oh": last_matmul,
             "OC": out_copy, "OCa": out_copy_first, "OCb": out_copy_last, "OB": out_round, "OQ": out_quant,
-            "BC": spread_matmul, "BCs": spread_copy,
+            "W": keep_warm, "BC": spread_matmul, "BCs": spread_copy,
             "Z": lambda n: z_matmul(n // 2, n % 2), "ZE": lambda n: z_affine(n // 2, n % 2),
         }
         for name, index in ORDER:

@@ -20,47 +20,45 @@ P = 128
 PACK = 4
 PASSES = 2
 BANK = 512
+BANKS = 8
 TILES = B * PACK
 PAIRS = TILES // 2
-ROTATING_BANKS = 8
-RELU_ON_VECTOR = ()
-LAST_RELU_ON_VECTOR = (0, 1,)
-H_COPY_ON_VECTOR = (9, 5, 2,)
-ROUND_ON_VECTOR = (3, 2,)
-GATE_ON_GPSIMD = (7, 5, 6,)
-STEPPED_TURN = (0, 2, 3, 5, 9, 10, 12, 14, 15,)
-WARM_MATMULS = 4
-ORDER = [
-    ("HT", 0), ("HT", 1), ("HC", 0), ("W", 0), ("HC", 1), ("HT", 2), ("HQ", 0), ("HT", 3), ("HC", 2),
-    ("BC", 0), ("VV", 0), ("HC", 3), ("BCs", 0), ("HT", 4), ("HQ", 1), ("TV", 0), ("HT", 5), ("HC", 4),
-    ("G1", 0), ("HT", 6), ("HT", 7), ("HC", 5), ("HC", 6), ("VV", 1), ("HQ", 2), ("HC", 7), ("UU", 0),
-    ("TV", 1), ("HQ", 3), ("VV", 2), ("TU", 0), ("G1", 1), ("HT", 8), ("TV", 2), ("HT", 9), ("G2", 0),
-    ("HC", 8), ("G2", 1), ("HT", 10), ("HC", 9), ("VV", 3), ("HC", 10), ("G1", 2), ("UU", 1), ("TV", 3),
-    ("HQ", 4), ("UU", 2), ("TU", 1), ("G1", 3), ("VV", 4), ("TU", 2), ("G2", 2), ("UU", 3), ("G2", 3),
-    ("UU", 4), ("G2", 4), ("TU", 3), ("HT", 11), ("G2", 5), ("TV", 4), ("HT", 12), ("G2", 6), ("HC", 11),
-    ("HT", 13), ("G2", 7), ("TU", 4), ("HT", 14), ("M4", 0), ("G1", 4), ("EA", 0), ("HC", 12), ("HT", 15),
-    ("HQ", 5), ("HC", 13), ("Z", 0), ("MX", 0), ("HC", 14), ("G2", 8), ("VV", 5), ("EX", 0), ("G2", 9),
-    ("Z", 1), ("EX", 1), ("HC", 15), ("HQ", 6), ("EB", 0), ("Z", 2), ("TV", 5), ("RC", 0), ("HQ", 7),
-    ("UU", 5), ("AM", 0), ("Z", 3), ("G1", 5), ("ZE", 0), ("TU", 5), ("VV", 6), ("ZE", 1), ("Z", 4),
-    ("ZE", 2), ("TV", 6), ("UU", 6), ("G2", 10), ("VV", 7), ("G2", 11), ("Z", 5), ("G1", 6), ("ZE", 3),
-    ("TV", 7), ("Z", 6), ("ZE", 4), ("TU", 6), ("Z", 7), ("ZE", 5), ("AM", 1), ("Z", 8), ("G1", 7), ("ZE", 6),
-    ("UU", 7), ("ZE", 7), ("Z", 9), ("TU", 7), ("Z", 10), ("ZE", 8), ("PT", 0), ("ZE", 9), ("PT", 1),
-    ("G2", 12), ("PT", 2), ("PR", 0), ("G2", 13), ("PT", 3), ("G2", 14), ("PR", 1), ("Z", 11), ("G2", 15),
-    ("Z", 12), ("ZE", 10), ("PR", 2), ("Z", 13), ("ZE", 11), ("Z", 14), ("M4", 1), ("ZE", 12), ("PR", 3),
-    ("PT", 4), ("EA", 1), ("ZE", 13), ("PT", 5), ("PR", 4), ("MX", 1), ("PT", 6), ("PQ", 0), ("Z", 15),
-    ("ZE", 14), ("EX", 2), ("Z", 16), ("EX", 3), ("PR", 5), ("PQ", 1), ("EB", 1), ("Z", 17), ("RC", 1),
-    ("ZE", 15), ("Z", 18), ("AM", 2), ("PR", 6), ("Z", 19), ("PQ", 2), ("Z", 20), ("ZE", 16), ("AM", 3),
-    ("Z", 21), ("ZE", 17), ("Z", 22), ("ZE", 18), ("PT", 7), ("PT", 8), ("ZE", 19), ("PR", 7), ("O", 0),
-    ("Z", 23), ("ZE", 20), ("O", 1), ("O", 2), ("ZE", 21), ("PR", 8), ("Z", 24), ("ZE", 22), ("O", 3),
-    ("Z", 25), ("OC", 0), ("ZE", 23), ("PT", 9), ("PT", 10), ("ZE", 24), ("OB", 0), ("PT", 11), ("PQ", 3),
-    ("PR", 9), ("Z", 26), ("ZE", 25), ("Z", 27), ("PR", 10), ("ZE", 26), ("Z", 28), ("ZE", 27), ("Z", 29),
-    ("PR", 11), ("ZE", 28), ("PT", 12), ("PT", 13), ("PQ", 4), ("PR", 12), ("O", 4), ("Z", 30), ("ZE", 29),
-    ("O", 5), ("Z", 31), ("PQ", 5), ("PR", 13), ("O", 6), ("ZE", 30), ("O", 7), ("PT", 14), ("OC", 1),
-    ("ZE", 31), ("PTh", 0), ("PR", 14), ("PQ", 6), ("PTh", 1), ("O", 8), ("PRh", 0), ("O", 9), ("O", 10),
-    ("PRh", 1), ("O", 11), ("OB", 1), ("O", 12), ("PQ1", 14), ("O", 13), ("PQh", 0), ("OC", 2), ("O", 14),
-    ("PQh", 1), ("Oh", 0), ("OQ", 0), ("Oh", 1), ("OCa", 0), ("OB", 2), ("OCb", 0), ("OQ", 1), ("OB", 3),
-    ("OQ", 2), ("OQ", 3),
-]
+LAST = TILES - 1
+WORK_BUFS = 4
+PRE_BUFS = 8
+
+COPY_H_ON_VECTOR = (2, 5, 8)
+WEIGH_ON_GPSIMD = (5, 6, 7)
+ROUND_ON_VECTOR = (2, 3)
+STEPPED_TURN = (0, 3, 5, 10, 12, 14, 15)
+
+ORDER = """
+turn_h:0 turn_h:1 copy_h:0 turn_h:2 copy_h:1 turn_h:3 quantise_h:0 copy_h:2 spread_wa:0 copy_h:3 matmul_v:0
+halve_wa:0 quantise_h:1 turn_h:4 tanh_v:0 weigh_v:0 turn_h:5 copy_h:4 turn_h:6 copy_h:5 turn_h:7 copy_h:6
+quantise_h:2 matmul_v:1 copy_h:7 matmul_u:0 tanh_v:1 quantise_h:3 matmul_v:2 tanh_u:0 weigh_v:1 turn_h:8 tanh_v:2
+score:0 turn_h:9 score:1 turn_h:10 copy_h:8 copy_h:9 matmul_v:3 weigh_v:2 matmul_u:1 quantise_h:4 tanh_v:3
+matmul_u:2 tanh_u:1 weigh_v:3 matmul_u:3 tanh_u:2 score:2 matmul_v:4 score:3 tanh_u:3 matmul_u:4 score:4 copy_h:10
+score:5 turn_h:11 tanh_v:4 score:6 turn_h:12 score:7 copy_h:11 turn_h:13 copy_h:12 min_rows:0 turn_h:14 weigh_v:4
+copy_h:13 spread_min:0 quantise_h:5 turn_h:15 tanh_u:4 min_bags:0 matmul_z:0 copy_h:14 score:8 matmul_v:5 exponent:0
+score:9 exponent:1 matmul_z:1 copy_h:15 quantise_h:6 mean_bags:0 tanh_v:5 matmul_z:2 invert:0 quantise_h:7
+normalise:0 matmul_v:6 weigh_v:5 affine:0 matmul_u:5 affine:1 matmul_z:3 tanh_u:5 affine:2 matmul_u:6 tanh_v:6
+matmul_z:4 score:10 score:11 matmul_v:7 weigh_v:6 affine:3 matmul_z:5 tanh_v:7 affine:4 matmul_z:6 tanh_u:6 affine:5
+matmul_z:7 weigh_v:7 normalise:1 matmul_u:7 affine:6 matmul_z:8 affine:7 tanh_u:7 matmul_z:9 affine:8 matmul_z:10
+score:12 turn_p:0 score:13 turn_p:1 affine:9 relu_p:0 turn_p:2 affine:10 turn_p:3 score:14 matmul_z:11 relu_p:1
+score:15 matmul_z:12 affine:11 relu_p:2 matmul_z:13 min_rows:1 affine:12 matmul_z:14 affine:13 relu_p:3 spread_min:1
+turn_p:4 min_bags:1 turn_p:5 quantise_p:0 relu_p:4 turn_p:6 affine:14 matmul_z:15 exponent:2 quantise_p:1
+matmul_z:16 exponent:3 relu_p:5 mean_bags:1 matmul_z:17 invert:1 affine:15 normalise:2 matmul_z:18 relu_p:6
+affine:16 matmul_z:19 matmul_z:20 affine:17 matmul_z:21 affine:18 turn_p:7 quantise_p:2 turn_p:8 relu_p:7 affine:19
+matmul_z:22 affine:20 matmul_out:0 matmul_z:23 relu_p:8 affine:21 matmul_out:1 matmul_out:2 matmul_z:24 affine:22
+normalise:3 matmul_out:3 matmul_z:25 affine:23 store_out:0 turn_p:9 affine:24 turn_p:10 round_out:0 quantise_p:3
+turn_p:11 relu_p:9 affine:25 matmul_z:26 matmul_z:27 relu_p:10 affine:26 matmul_z:28 affine:27 turn_p:12 relu_p:11
+affine:28 turn_p:13 quantise_p:4 matmul_z:29 relu_p:12 matmul_out:4 matmul_z:30 affine:29 relu_p:13 matmul_z:31
+quantise_p:5 matmul_out:5 matmul_out:6 affine:30 matmul_out:7 turn_p:14 store_out:1 affine:31 turn_last:0 relu_p:14
+quantise_p:6 turn_last:1 matmul_out:8 relu_last:0 matmul_out:9 matmul_out:10 relu_last:1 matmul_out:11 round_out:1
+matmul_out:12 quantise_p:7 matmul_out:13 quantise_last:0 store_out:2 matmul_out:14 quantise_last:1 matmul_last:0
+quantise_out:0 matmul_last:1 store_out:3 round_out:2 store_last:3 quantise_out:1 round_out:3 quantise_out:2
+quantise_out:3
+"""
 
 
 def tile_additivemilpatchcontributionlogits_x2_kernel(
@@ -70,14 +68,15 @@ def tile_additivemilpatchcontributionlogits_x2_kernel(
     nc = tc.nc
     with ExitStack() as ctx:
         keep = ctx.enter_context(tc.tile_pool(name="keep", bufs=1))
-        work = ctx.enter_context(tc.tile_pool(name="work", bufs=4))
+        work = ctx.enter_context(tc.tile_pool(name="work", bufs=WORK_BUFS))
         psum = ctx.enter_context(tc.psum_pool(name="psum", bufs=1))
-        ctx.enter_context(tc.manual_schedule(engines={mybir.EngineType.PE, mybir.EngineType.SP, mybir.EngineType.Activation, mybir.EngineType.DVE, mybir.EngineType.Pool}))
+        ctx.enter_context(tc.manual_schedule())
 
         banks_taken = []
+        held = {}
 
         def next_bank():
-            k = len(banks_taken) % ROTATING_BANKS
+            k = len(banks_taken) % BANKS
             banks_taken.append(k)
             return psum.tile([P, BANK], F32, name="bank%d" % k)
 
@@ -91,11 +90,11 @@ def tile_additivemilpatchcontributionlogits_x2_kernel(
             src = words.rearrange("g p n t -> p g (n t)").bitcast(I32)
             nc.sync.dma_start(out=codes[:, g0:g1, :].bitcast(I32), in_=src[:, g0:g1, :])
 
-        def load_scales(queue, scales, rows):
-            for q in range(4):
-                queue.dma_start(
-                    out=scales[32 * q : 32 * q + 4, :, :].bitcast(I32),
-                    in_=rows[:, 4 * q : 4 * q + 4, :].rearrange("g r n -> r g n").bitcast(I32),
+        def load_scales(scales, rows):
+            for quad in range(4):
+                nc.sync.dma_start(
+                    out=scales[32 * quad : 32 * quad + 4, :, :].bitcast(I32),
+                    in_=rows[:, 4 * quad : 4 * quad + 4, :].rearrange("g r n -> r g n").bitcast(I32),
                 )
 
         h_raw = [keep.tile([P, PACK, D], BF16, name="h_raw%d" % b) for b in range(B)]
@@ -103,71 +102,66 @@ def tile_additivemilpatchcontributionlogits_x2_kernel(
         def load_h(b, t0, t1):
             nc.sync.dma_start(out=h_raw[b][:, t0:t1, :], in_=h[b].rearrange("(p t) d -> p t d", t=PACK)[:, t0:t1, :])
 
-        warm = keep.tile([P, BANK], BF16)
-        nc.gpsimd.memset(warm[:], 0.0)
-        warm_bank = next_bank()
-        for n in range(WARM_MATMULS):
-            nc.tensor.matmul(warm_bank[:], lhsT=warm[:, 0:P], rhs=warm[:], start=True, stop=True)
         ident = keep.tile([P, P], F32)
         make_identity(nc, ident[:])
-        wv_c, wv_s = weight_tiles("wv", A)
-        wu_c, wu_s = weight_tiles("wu", A)
+        wv_codes, wv_plane = weight_tiles("wv", A)
+        zeros = keep.tile([P, P], BF16)
+        nc.vector.memset(zeros[:], 0.0)
         wa_row = keep.tile([P, A], BF16)
         nc.vector.memset(wa_row[:], 0.0)
-        w1_c, w1_s = weight_tiles("w1", F)
-        w2_c, w2_s = weight_tiles("w2", C)
-
+        wu_codes, wu_plane = weight_tiles("wu", A)
+        w1_codes, w1_plane = weight_tiles("w1", F)
+        w2_codes, w2_plane = weight_tiles("w2", C)
         ones = keep.tile([P, P], BF16)
-        nc.scalar.activation(out=ones[:], in_=warm[:, 0:P], func=ACT.Exp)
+        nc.scalar.activation(out=ones[:], in_=zeros[:], func=ACT.Exp)
         per_patch = keep.tile([P, P], F32)
         nc.gpsimd.memset(per_patch[:], 1.0 / N)
         nc.gpsimd.dma_start(out=wa_row[0:1, :], in_=wa.unsqueeze(0))
+
         load_h(0, 0, 1)
         load_h(0, 1, 2)
         load_h(0, 2, 4)
-        load_scales(nc.sync, wv_s, wv_scales)
-        load_codes(wv_c, wv_words, 0, 2)
+        load_scales(wv_plane, wv_scales)
+        load_codes(wv_codes, wv_words, 0, PASSES)
         load_h(1, 0, 2)
         load_h(1, 2, 4)
-        load_scales(nc.sync, wu_s, wu_scales)
-        load_codes(wu_c, wu_words, 0, 2)
-        for j in range(4, PAIRS):
-            load_h(j // 2, 2 * (j % 2), 2 * (j % 2) + 2)
-        load_scales(nc.sync, w1_s, w1_scales)
-        load_codes(w1_c, w1_words, 0, 1)
-        load_codes(w1_c, w1_words, 1, 2)
+        load_scales(wu_plane, wu_scales)
+        load_codes(wu_codes, wu_words, 0, PASSES)
+        for b in range(2, B):
+            load_h(b, 0, 2)
+            load_h(b, 2, 4)
+        load_scales(w1_plane, w1_scales)
+        load_codes(w1_codes, w1_words, 0, 1)
+        load_codes(w1_codes, w1_words, 1, 2)
         b1_all = keep.tile([P, PASSES, BANK], BF16)
         nc.sync.dma_start(out=b1_all[:].rearrange("p g f -> p (g f)"), in_=b1.partition_broadcast(P))
-        load_scales(nc.sync, w2_s, w2_scales)
-        load_codes(w2_c, w2_words, 0, 2)
+        load_scales(w2_plane, w2_scales)
+        load_codes(w2_codes, w2_words, 0, PASSES)
 
         wa_all = keep.tile([P, A], F32)
         h_codes = [keep.tile([P, 2, PASSES * P], U32, name="h_codes%d" % j, align_bytes=64) for j in range(PAIRS)]
         h_scales = [keep.tile([P, 2, PASSES * P], U8, name="h_scales%d" % j, align_bytes=64) for j in range(PAIRS)]
         neg_e = [keep.tile([P, 2, PACK], F32, name="neg_e%d" % k) for k in range(B // 2)]
-        part_min = [keep.tile([P, 2], F32, name="part_min%d" % k) for k in range(B // 2)]
+        row_min = [keep.tile([P, 2], F32, name="row_min%d" % k) for k in range(B // 2)]
         bag_min = [keep.tile([P, 2], F32, name="bag_min%d" % k) for k in range(B // 2)]
-        part_sum = [keep.tile([P, 2], F32, name="part_sum%d" % k) for k in range(B // 2)]
+        row_sum = [keep.tile([P, 2], F32, name="row_sum%d" % k) for k in range(B // 2)]
         inverse = [keep.tile([P, 2], F32, name="inverse%d" % k) for k in range(B // 2)]
         expo = [keep.tile([P, PACK], F32, name="expo%d" % b) for b in range(B)]
         attn = [keep.tile([P, PACK], F32, name="attn%d" % b) for b in range(B)]
         out_codes = keep.tile([P, B * C], U32, align_bytes=64)
         out_scales = keep.tile([P, B * C], U8, align_bytes=64)
-        held = {}
 
-        def spread_matmul(k):
+        def spread_wa(index):
             bank = next_bank()
             nc.tensor.matmul(bank[:, 0:A], lhsT=ones[:], rhs=wa_row[:], start=True, stop=True)
-            held["row_bank", k] = bank
+            held["wa_bank", index] = bank
 
-        def keep_warm(k):
-            for n in range(2):
-                nc.tensor.matmul(warm_bank[:], lhsT=warm[:, 0:P], rhs=warm[:], start=True, stop=True)
+        def halve_wa(index):
+            nc.vector.tensor_scalar(
+                out=wa_all[:], in0=held["wa_bank", index][:, 0:A], scalar1=-0.5, scalar2=None, op0=ALU.mult
+            )
 
-        def spread_copy(k):
-            nc.vector.tensor_scalar(out=wa_all[:], in0=held["row_bank", k][:, 0:A], scalar1=-0.5, scalar2=None, op0=ALU.mult)
-
-        def h_turn(i):
+        def turn_h(i):
             words = h_raw[i // PACK][:, i % PACK, :].bitcast(F32)
             bank = next_bank()
             for u in range(2):
@@ -176,17 +170,17 @@ def tile_additivemilpatchcontributionlogits_x2_kernel(
                     nc.tensor.transpose(bank[:, col : col + P], words[:, 256 * g + u : 256 * (g + 1) : 2], ident[:])
             held["h_bank", i] = bank
 
-        def h_copy(i):
+        def copy_h(i):
             if ("h_grouped", i // 2) not in held:
                 held["h_grouped", i // 2] = work.tile([P, 2, D], BF16, name="h_grouped", align_bytes=64)
             dst = held["h_grouped", i // 2][:, i % 2, :].bitcast(F32).rearrange("p (q u) -> p q u", u=2)
             src = held["h_bank", i][:].rearrange("p (u q) -> p q u", u=2)
-            if i in H_COPY_ON_VECTOR:
+            if i in COPY_H_ON_VECTOR:
                 nc.vector.tensor_copy(out=dst, in_=src)
             else:
                 nc.scalar.copy(out=dst, in_=src)
 
-        def h_quant(j):
+        def quantise_h(j):
             nc.vector.quantize_mx(
                 out=h_codes[j][:].rearrange("p s q -> p (s q)").bitcast(FP8X4),
                 scales=h_scales[j][:].rearrange("p s q -> p (s q)"),
@@ -195,9 +189,10 @@ def tile_additivemilpatchcontributionlogits_x2_kernel(
 
         def times_h(out, i, codes, scales, cols):
             for g in range(PASSES):
-                k = slice(g * P, (g + 1) * P)
+                patches = slice(g * P, (g + 1) * P)
                 nc.tensor.matmul_mx(
-                    out=out, lhsT=h_codes[i // 2][:, i % 2, k].bitcast(FP8X4), lhsT_scale=h_scales[i // 2][:, i % 2, k],
+                    out=out, lhsT=h_codes[i // 2][:, i % 2, patches].bitcast(FP8X4),
+                    lhsT_scale=h_scales[i // 2][:, i % 2, patches],
                     rhs=codes[:, g, cols].bitcast(FP8X4), rhs_scale=scales[:, g, cols],
                     start=(g == 0), stop=(g == PASSES - 1),
                 )
@@ -208,50 +203,51 @@ def tile_additivemilpatchcontributionlogits_x2_kernel(
                 times_h(bank[:, s * A : (s + 1) * A], 2 * j + s, codes, scales, slice(0, A))
             held[key, j] = bank
 
-        def u_matmul(j):
-            gate_matmul(j, "u_bank", wu_c, wu_s)
+        def matmul_u(j):
+            gate_matmul(j, "u_bank", wu_codes, wu_plane)
 
-        def v_matmul(j):
-            gate_matmul(j, "v_bank", wv_c, wv_s)
+        def matmul_v(j):
+            gate_matmul(j, "v_bank", wv_codes, wv_plane)
 
-        def u_tanh(j):
-            tanh_u = work.tile([P, 2, A], F32, name="tanh_u")
-            nc.scalar.activation(out=tanh_u[:].rearrange("p s a -> p (s a)"), in_=held["u_bank", j][:], func=ACT.Tanh, scale=0.5)
-            held["tanh_u", j] = tanh_u
-
-        def v_tanh(j):
-            tanh_v = work.tile([P, 2, A], F32, name="tanh_v")
-            nc.scalar.activation(out=tanh_v[:].rearrange("p s a -> p (s a)"), in_=held["v_bank", j][:], func=ACT.Tanh)
-            held["tanh_v", j] = tanh_v
-
-        def gate_weigh(j):
-            gate = work.tile([P, 2, A], F32, name="gate")
-            engine = nc.gpsimd if j in GATE_ON_GPSIMD else nc.vector
-            engine.tensor_tensor(
-                out=gate[:], in0=held["tanh_v", j][:], in1=wa_all[:].unsqueeze(1).to_broadcast([P, 2, A]), op=ALU.mult
+        def tanh_u(j):
+            half_u = work.tile([P, 2, A], F32, name="tanh_u")
+            nc.scalar.activation(
+                out=half_u[:].rearrange("p s a -> p (s a)"), in_=held["u_bank", j][:], func=ACT.Tanh, scale=0.5
             )
-            held["gate", j] = gate
+            held["tanh_u", j] = half_u
+
+        def tanh_v(j):
+            whole_v = work.tile([P, 2, A], F32, name="tanh_v")
+            nc.scalar.activation(out=whole_v[:].rearrange("p s a -> p (s a)"), in_=held["v_bank", j][:], func=ACT.Tanh)
+            held["tanh_v", j] = whole_v
+
+        def weigh_v(j):
+            weighed = work.tile([P, 2, A], F32, name="weighed")
+            engine = nc.gpsimd if j in WEIGH_ON_GPSIMD else nc.vector
+            engine.tensor_tensor(
+                out=weighed[:], in0=held["tanh_v", j][:], in1=wa_all[:].unsqueeze(1).to_broadcast([P, 2, A]), op=ALU.mult
+            )
+            held["weighed", j] = weighed
 
         def score(i):
             terms = work.tile([P, A], F32, name="terms")
             b, t = divmod(i, PACK)
             nc.vector.scalar_tensor_tensor(
                 out=terms[:], in0=held["tanh_u", i // 2][:, i % 2, :], scalar=1.0,
-                in1=held["gate", i // 2][:, i % 2, :], op0=ALU.add, op1=ALU.mult,
+                in1=held["weighed", i // 2][:, i % 2, :], op0=ALU.add, op1=ALU.mult,
                 accum_out=neg_e[b // 2][:, b % 2, t : t + 1],
             )
 
-        def min_local(k):
-            nc.vector.tensor_reduce(out=part_min[k][:], in_=neg_e[k][:], axis=AXIS.X, op=ALU.min)
+        def min_rows(k):
+            nc.vector.tensor_reduce(out=row_min[k][:], in_=neg_e[k][:], axis=AXIS.X, op=ALU.min)
 
-
-        def min_spread(k):
+        def spread_min(k):
             bank = next_bank()
             for s in range(2):
-                nc.tensor.transpose(bank[:, s * P : (s + 1) * P], part_min[k][:, s : s + 1].to_broadcast([P, P]), ident[:])
+                nc.tensor.transpose(bank[:, s * P : (s + 1) * P], row_min[k][:, s : s + 1].to_broadcast([P, P]), ident[:])
             held["min_bank", k] = bank
 
-        def min_all(k):
+        def min_bags(k):
             spread = held["min_bank", k][:, 0 : 2 * P].rearrange("p (s n) -> p s n", s=2)
             nc.vector.tensor_reduce(out=bag_min[k][:], in_=spread, axis=AXIS.X, op=ALU.min)
 
@@ -259,14 +255,13 @@ def tile_additivemilpatchcontributionlogits_x2_kernel(
             k, s = divmod(b, 2)
             nc.scalar.activation(
                 out=expo[b][:], in_=neg_e[k][:, s, :], func=ACT.Exp, scale=-1.0, bias=bag_min[k][:, s : s + 1],
-                accum_out=part_sum[k][:, s : s + 1],
+                accum_out=row_sum[k][:, s : s + 1],
             )
 
-        def mean_matmul(k):
+        def mean_bags(k):
             bank = next_bank()
-            nc.tensor.matmul(bank[:, 0:2], lhsT=per_patch[:], rhs=part_sum[k][:], start=True, stop=True)
+            nc.tensor.matmul(bank[:, 0:2], lhsT=per_patch[:], rhs=row_sum[k][:], start=True, stop=True)
             held["mean_bank", k] = bank
-
 
         def invert(k):
             nc.vector.reciprocal(out=inverse[k][:], in_=held["mean_bank", k][:, 0:2])
@@ -275,16 +270,18 @@ def tile_additivemilpatchcontributionlogits_x2_kernel(
             k, s = divmod(b, 2)
             nc.scalar.activation(out=attn[b][:], in_=expo[b][:], func=ACT.Copy, scale=inverse[k][:, s : s + 1])
 
-        def z_matmul(i, half):
+        def matmul_z(n):
+            i, g = divmod(n, PASSES)
             bank = next_bank()
-            times_h(bank[:], i, w1_c, w1_s, slice(half * BANK, (half + 1) * BANK))
-            held["z_bank", i, half] = bank
+            times_h(bank[:], i, w1_codes, w1_plane, slice(g * BANK, (g + 1) * BANK))
+            held["z_bank", n] = bank
 
-        def z_affine(i, half):
-            if half == 0:
-                held["pre", i] = work.tile([P, PASSES, BANK], BF16, name="pre", bufs=8)
+        def affine(n):
+            i, g = divmod(n, PASSES)
+            if g == 0:
+                held["pre", i] = work.tile([P, PASSES, BANK], BF16, name="pre", bufs=PRE_BUFS)
             b, t = divmod(i, PACK)
-            z, bias, pre = held["z_bank", i, half][:], b1_all[:, half, :], held["pre", i][:, half, :]
+            z, bias, pre = held["z_bank", n][:], b1_all[:, g, :], held["pre", i][:, g, :]
             if i in STEPPED_TURN:
                 parts = [(z, bias, pre)]
             else:
@@ -296,99 +293,96 @@ def tile_additivemilpatchcontributionlogits_x2_kernel(
                     out=pre_part, in0=z_part, scalar=attn[b][:, t : t + 1], in1=bias_part, op0=ALU.mult, op1=ALU.add
                 )
 
-        def turn_p(i, halves):
+        def turn_passes(i, passes):
             words = held["pre", i][:].rearrange("p g f -> p (g f)").bitcast(F32)
             bank = next_bank()
-            for n, g in enumerate(halves):
+            for place, g in enumerate(passes):
                 for u in range(2):
-                    col = (u * len(halves) + n) * P
+                    col = (u * len(passes) + place) * P
                     if i in STEPPED_TURN:
                         src = words[:, 256 * g + u : 256 * (g + 1) : 2]
                     else:
                         src = words[:, (g * 2 + u) * P : (g * 2 + u + 1) * P]
                     nc.tensor.transpose(bank[:, col : col + P], src, ident[:])
-            held["p_bank", i, halves[0]] = bank
+            held["p_bank", i, passes[0]] = bank
 
-        def p_turn(i):
-            turn_p(i, (0, 1))
+        def turn_p(i):
+            turn_passes(i, (0, 1))
 
-        def last_turn(g):
-            turn_p(TILES - 1, (g,))
+        def turn_last(g):
+            turn_passes(LAST, (g,))
 
-        def relu_p(i, first, count, on_vector):
+        def relu_passes(i, first, count, on_vector):
             if ("p_grouped", i // 2) not in held:
                 held["p_grouped", i // 2] = work.tile([P, 2, F], BF16, name="p_grouped", align_bytes=64)
             cols = slice(first * BANK, (first + count) * BANK)
             dst = held["p_grouped", i // 2][:, i % 2, cols].rearrange("p (q u e) -> p q u e", u=2, e=2)
-            src = held["p_bank", i, first][:].bitcast(BF16)[:, 0 : count * BANK].rearrange("p (u q e) -> p q u e", u=2, e=2)
+            values = held["p_bank", i, first][:].bitcast(BF16)[:, 0 : count * BANK]
+            src = values.rearrange("p (u q e) -> p q u e", u=2, e=2)
             if on_vector:
                 nc.vector.tensor_scalar(out=dst, in0=src, scalar1=0.0, scalar2=None, op0=ALU.max)
             else:
                 nc.scalar.activation(out=dst, in_=src, func=ACT.Relu)
 
-        def p_relu(i):
-            relu_p(i, 0, 2, i in RELU_ON_VECTOR)
+        def relu_p(i):
+            relu_passes(i, 0, PASSES, on_vector=False)
 
-        def last_relu(g):
-            relu_p(TILES - 1, g, 1, g in LAST_RELU_ON_VECTOR)
+        def relu_last(g):
+            relu_passes(LAST, g, 1, on_vector=True)
 
-        def quant_p(j, first, count):
+        def quantise_passes(j, first, count):
             if first == 0:
-                codes = work.tile([P, 2 * PASSES * P], U32, name="p_codes", align_bytes=64, bufs=8)
-                scales = work.tile([P, 2 * PASSES * P], U8, name="p_scales", align_bytes=64, bufs=8)
-                held["p_quant", j] = (codes, scales)
-            codes, scales = held["p_quant", j]
+                codes = work.tile([P, 2 * PASSES * P], U32, name="p_codes", align_bytes=64, bufs=PRE_BUFS)
+                scales = work.tile([P, 2 * PASSES * P], U8, name="p_scales", align_bytes=64, bufs=PRE_BUFS)
+                held["p_quantised", j] = (codes, scales)
+            codes, scales = held["p_quantised", j]
             cols = slice(first * P, (first + count) * P)
             src = held["p_grouped", j][:].rearrange("p s f -> p (s f)")[:, first * BANK : (first + count) * BANK]
             nc.vector.quantize_mx(out=codes[:, cols].bitcast(FP8X4), scales=scales[:, cols], in_=src)
 
-        def p_quant(j):
-            quant_p(j, 0, 4)
+        def quantise_p(j):
+            quantise_passes(j, 0, 2 * PASSES if j < PAIRS - 1 else PASSES)
 
-        def p_quant_one(i):
-            quant_p(i // 2, 0, 2)
-
-        def last_quant(g):
-            quant_p(PAIRS - 1, 2 + g, 1)
+        def quantise_last(g):
+            quantise_passes(PAIRS - 1, PASSES + g, 1)
 
         def out_pass(out, i, g):
-            codes, scales = held["p_quant", i // 2]
-            k = slice((2 * (i % 2) + g) * P, (2 * (i % 2) + g + 1) * P)
+            codes, scales = held["p_quantised", i // 2]
+            place = PASSES * (i % 2) + g
+            patches = slice(place * P, (place + 1) * P)
             nc.tensor.matmul_mx(
-                out=out, lhsT=codes[:, k].bitcast(FP8X4), lhsT_scale=scales[:, k],
-                rhs=w2_c[:, g, :].bitcast(FP8X4), rhs_scale=w2_s[:, g, :],
+                out=out, lhsT=codes[:, patches].bitcast(FP8X4), lhsT_scale=scales[:, patches],
+                rhs=w2_codes[:, g, :].bitcast(FP8X4), rhs_scale=w2_plane[:, g, :],
                 start=(g == 0), stop=(g == PASSES - 1),
             )
 
-        def out_matmul(i):
+        def matmul_out(i):
             b, t = divmod(i, PACK)
             if t == 0:
                 held["out_bank", b] = next_bank()
             for g in range(PASSES):
                 out_pass(held["out_bank", b][:, t * C : (t + 1) * C], i, g)
 
-        def last_matmul(g):
+        def matmul_last(g):
             if g == 0:
                 held["last_bank"] = next_bank()
-            out_pass(held["last_bank"][:, 0:C], TILES - 1, g)
+            out_pass(held["last_bank"][:, 0:C], LAST, g)
 
-        def copy_out(b, src, t0, t1):
+        def store_tiles(b, src, t0, t1):
             if ("result", b) not in held:
                 held["result", b] = work.tile([P, PACK * C], F32, name="result")
             cols = slice(t0 * C, t1 * C)
             nc.scalar.copy(out=held["result", b][:, cols], in_=src)
             nc.sync.dma_start(out=out_0[b].rearrange("(p t) c -> p (t c)", t=PACK)[:, cols], in_=held["result", b][:, cols])
 
-        def out_copy(b):
-            copy_out(b, held["out_bank", b][:], 0, PACK)
+        def store_out(b):
+            tiles = PACK if b < B - 1 else PACK - 1
+            store_tiles(b, held["out_bank", b][:, 0 : tiles * C], 0, tiles)
 
-        def out_copy_first(b):
-            copy_out(B - 1, held["out_bank", B - 1][:, 0 : (PACK - 1) * C], 0, PACK - 1)
+        def store_last(b):
+            store_tiles(b, held["last_bank"][:, 0:C], PACK - 1, PACK)
 
-        def out_copy_last(b):
-            copy_out(B - 1, held["last_bank"][:, 0:C], PACK - 1, PACK)
-
-        def out_round(b):
+        def round_out(b):
             grouped = work.tile([P, C, PACK], BF16, name="out_grouped", align_bytes=64)
             if b in ROUND_ON_VECTOR:
                 nc.vector.tensor_copy(out=grouped[:], in_=held["result", b][:].rearrange("p (t c) -> p c t", t=PACK))
@@ -396,7 +390,7 @@ def tile_additivemilpatchcontributionlogits_x2_kernel(
                 nc.scalar.copy(out=grouped[:], in_=held["out_bank", b][:].rearrange("p (t c) -> p c t", t=PACK))
             held["out_grouped", b] = grouped
 
-        def out_quant(b):
+        def quantise_out(b):
             cols = slice(b * C, (b + 1) * C)
             nc.vector.quantize_mx(
                 out=out_codes[:, cols].bitcast(FP8X4), scales=out_scales[:, cols],
@@ -406,22 +400,25 @@ def tile_additivemilpatchcontributionlogits_x2_kernel(
                 out=out_1[0].rearrange("p m t -> p (m t)").bitcast(I32)[:, cols], in_=out_codes[:, cols].bitcast(I32)
             )
 
-        def store_scales():
-            for q in range(4):
-                queue = nc.sync if q % 2 == 0 else nc.scalar
-                queue.dma_start(
-                    out=out_2[0, 4 * q : 4 * q + 4, :].bitcast(I32), in_=out_scales[32 * q : 32 * q + 4, :].bitcast(I32)
-                )
-
         steps = {
-            "HT": h_turn, "HC": h_copy, "HQ": h_quant, "UU": u_matmul, "VV": v_matmul, "TU": u_tanh, "TV": v_tanh,
-            "G1": gate_weigh, "G2": score, "M4": min_local, "EA": min_spread, "MX": min_all, "EX": exponent,
-            "EB": mean_matmul, "RC": invert, "AM": normalise, "PT": p_turn, "PTh": last_turn, "PR": p_relu,
-            "PRh": last_relu, "PQ": p_quant, "PQ1": p_quant_one, "PQh": last_quant, "O": out_matmul, "Oh": last_matmul,
-            "OC": out_copy, "OCa": out_copy_first, "OCb": out_copy_last, "OB": out_round, "OQ": out_quant,
-            "W": keep_warm, "BC": spread_matmul, "BCs": spread_copy,
-            "Z": lambda n: z_matmul(n // 2, n % 2), "ZE": lambda n: z_affine(n // 2, n % 2),
+            "spread_wa": spread_wa, "halve_wa": halve_wa,
+            "turn_h": turn_h, "copy_h": copy_h, "quantise_h": quantise_h,
+            "matmul_u": matmul_u, "matmul_v": matmul_v, "tanh_u": tanh_u, "tanh_v": tanh_v,
+            "weigh_v": weigh_v, "score": score,
+            "min_rows": min_rows, "spread_min": spread_min, "min_bags": min_bags, "exponent": exponent,
+            "mean_bags": mean_bags, "invert": invert, "normalise": normalise,
+            "matmul_z": matmul_z, "affine": affine,
+            "turn_p": turn_p, "relu_p": relu_p, "quantise_p": quantise_p, "matmul_out": matmul_out,
+            "turn_last": turn_last, "relu_last": relu_last, "quantise_last": quantise_last, "matmul_last": matmul_last,
+            "store_out": store_out, "store_last": store_last, "round_out": round_out, "quantise_out": quantise_out,
         }
-        for name, index in ORDER:
-            steps[name](index)
-        store_scales()
+        for entry in ORDER.split():
+            step, index = entry.split(":")
+            steps[step](int(index))
+
+        for quad in range(4):
+            queue = nc.sync if quad % 2 == 0 else nc.scalar
+            queue.dma_start(
+                out=out_2[0, 4 * quad : 4 * quad + 4, :].bitcast(I32),
+                in_=out_scales[32 * quad : 32 * quad + 4, :].bitcast(I32),
+            )

from contextlib import ExitStack

import concourse.mybir as mybir
from concourse.masks import make_identity

B, N, D, A, F, C = 4, 512, 1024, 256, 1024, 128
FLOPS = 2 * B * N * (2 * D * A + D * F + F * C)

F32 = mybir.dt.float32
BF16 = mybir.dt.bfloat16
I32 = mybir.dt.int32
U32 = mybir.dt.uint32
U8 = mybir.dt.uint8
FP8X4 = mybir.dt.float8_e4m3fn_x4
ACT = mybir.ActivationFunctionType
ALU = mybir.AluOpType
AXIS = mybir.AxisListType

P = 128
PACK = 4
PASSES = 2
BANK = 512
BANKS = 8
TILES = B * PACK
PAIRS = TILES // 2
LAST = TILES - 1
WORK_BUFS = 4
PRE_BUFS = 8

COPY_H_ON_VECTOR = (2, 5, 8)
WEIGH_ON_GPSIMD = (5, 6, 7)
ROUND_ON_VECTOR = (2, 3)
STEPPED_TURN = (0, 3, 5, 10, 12, 14, 15)

ORDER = """
turn_h:0 turn_h:1 copy_h:0 turn_h:2 copy_h:1 turn_h:3 quantise_h:0 copy_h:2 spread_wa:0 copy_h:3 matmul_v:0
halve_wa:0 quantise_h:1 turn_h:4 tanh_v:0 weigh_v:0 turn_h:5 copy_h:4 turn_h:6 copy_h:5 turn_h:7 copy_h:6
quantise_h:2 matmul_v:1 copy_h:7 matmul_u:0 tanh_v:1 quantise_h:3 matmul_v:2 tanh_u:0 weigh_v:1 turn_h:8 tanh_v:2
score:0 turn_h:9 score:1 turn_h:10 copy_h:8 copy_h:9 matmul_v:3 weigh_v:2 matmul_u:1 quantise_h:4 tanh_v:3
matmul_u:2 tanh_u:1 weigh_v:3 matmul_u:3 tanh_u:2 score:2 matmul_v:4 score:3 tanh_u:3 matmul_u:4 score:4 copy_h:10
score:5 turn_h:11 tanh_v:4 score:6 turn_h:12 score:7 copy_h:11 turn_h:13 copy_h:12 min_rows:0 turn_h:14 weigh_v:4
copy_h:13 spread_min:0 quantise_h:5 turn_h:15 tanh_u:4 min_bags:0 matmul_z:0 copy_h:14 score:8 matmul_v:5 exponent:0
score:9 exponent:1 matmul_z:1 copy_h:15 quantise_h:6 mean_bags:0 tanh_v:5 matmul_z:2 invert:0 quantise_h:7
normalise:0 matmul_v:6 weigh_v:5 affine:0 matmul_u:5 affine:1 matmul_z:3 tanh_u:5 affine:2 matmul_u:6 tanh_v:6
matmul_z:4 score:10 score:11 matmul_v:7 weigh_v:6 affine:3 matmul_z:5 tanh_v:7 affine:4 matmul_z:6 tanh_u:6 affine:5
matmul_z:7 weigh_v:7 normalise:1 matmul_u:7 affine:6 matmul_z:8 affine:7 tanh_u:7 matmul_z:9 affine:8 matmul_z:10
score:12 turn_p:0 score:13 turn_p:1 affine:9 relu_p:0 turn_p:2 affine:10 turn_p:3 score:14 matmul_z:11 relu_p:1
score:15 matmul_z:12 affine:11 relu_p:2 matmul_z:13 min_rows:1 affine:12 matmul_z:14 affine:13 relu_p:3 spread_min:1
turn_p:4 min_bags:1 turn_p:5 quantise_p:0 relu_p:4 turn_p:6 affine:14 matmul_z:15 exponent:2 quantise_p:1
matmul_z:16 exponent:3 relu_p:5 mean_bags:1 matmul_z:17 invert:1 affine:15 normalise:2 matmul_z:18 relu_p:6
affine:16 matmul_z:19 matmul_z:20 affine:17 matmul_z:21 affine:18 turn_p:7 quantise_p:2 turn_p:8 relu_p:7 affine:19
matmul_z:22 affine:20 matmul_out:0 matmul_z:23 relu_p:8 affine:21 matmul_out:1 matmul_out:2 matmul_z:24 affine:22
normalise:3 matmul_out:3 matmul_z:25 affine:23 store_out:0 turn_p:9 affine:24 turn_p:10 round_out:0 quantise_p:3
turn_p:11 relu_p:9 affine:25 matmul_z:26 matmul_z:27 relu_p:10 affine:26 matmul_z:28 affine:27 turn_p:12 relu_p:11
affine:28 turn_p:13 quantise_p:4 matmul_z:29 relu_p:12 matmul_out:4 matmul_z:30 affine:29 relu_p:13 matmul_z:31
quantise_p:5 matmul_out:5 matmul_out:6 affine:30 matmul_out:7 turn_p:14 store_out:1 affine:31 turn_last:0 relu_p:14
quantise_p:6 turn_last:1 matmul_out:8 relu_last:0 matmul_out:9 matmul_out:10 relu_last:1 matmul_out:11 round_out:1
matmul_out:12 quantise_p:7 matmul_out:13 quantise_last:0 store_out:2 matmul_out:14 quantise_last:1 matmul_last:0
quantise_out:0 matmul_last:1 store_out:3 round_out:2 store_last:3 quantise_out:1 round_out:3 quantise_out:2
quantise_out:3
"""


def tile_additivemilpatchcontributionlogits_x2_kernel(
    tc, h, wv_words, wv_scales, wu_words, wu_scales, wa, w1_words, w1_scales, b1, w2_words, w2_scales,
    out_0, out_1, out_2,
):
    nc = tc.nc
    with ExitStack() as ctx:
        keep = ctx.enter_context(tc.tile_pool(name="keep", bufs=1))
        work = ctx.enter_context(tc.tile_pool(name="work", bufs=WORK_BUFS))
        psum = ctx.enter_context(tc.psum_pool(name="psum", bufs=1))
        ctx.enter_context(tc.manual_schedule())

        banks_taken = []
        held = {}

        def next_bank():
            k = len(banks_taken) % BANKS
            banks_taken.append(k)
            return psum.tile([P, BANK], F32, name="bank%d" % k)

        def weight_tiles(name, width):
            codes = keep.tile([P, PASSES, width], U32, name=name + "_codes", align_bytes=64)
            scales = keep.tile([P, PASSES, width], U8, name=name + "_scales", align_bytes=64)
            nc.vector.memset(scales[:].bitcast(I32), 0)
            return codes, scales

        def load_codes(codes, words, g0, g1):
            src = words.rearrange("g p n t -> p g (n t)").bitcast(I32)
            nc.sync.dma_start(out=codes[:, g0:g1, :].bitcast(I32), in_=src[:, g0:g1, :])

        def load_scales(scales, rows):
            for quad in range(4):
                nc.sync.dma_start(
                    out=scales[32 * quad : 32 * quad + 4, :, :].bitcast(I32),
                    in_=rows[:, 4 * quad : 4 * quad + 4, :].rearrange("g r n -> r g n").bitcast(I32),
                )

        h_raw = [keep.tile([P, PACK, D], BF16, name="h_raw%d" % b) for b in range(B)]

        def load_h(b, t0, t1):
            nc.sync.dma_start(out=h_raw[b][:, t0:t1, :], in_=h[b].rearrange("(p t) d -> p t d", t=PACK)[:, t0:t1, :])

        ident = keep.tile([P, P], F32)
        make_identity(nc, ident[:])
        wv_codes, wv_plane = weight_tiles("wv", A)
        zeros = keep.tile([P, P], BF16)
        nc.vector.memset(zeros[:], 0.0)
        wa_row = keep.tile([P, A], BF16)
        nc.vector.memset(wa_row[:], 0.0)
        wu_codes, wu_plane = weight_tiles("wu", A)
        w1_codes, w1_plane = weight_tiles("w1", F)
        w2_codes, w2_plane = weight_tiles("w2", C)
        ones = keep.tile([P, P], BF16)
        nc.scalar.activation(out=ones[:], in_=zeros[:], func=ACT.Exp)
        per_patch = keep.tile([P, P], F32)
        nc.gpsimd.memset(per_patch[:], 1.0 / N)
        nc.gpsimd.dma_start(out=wa_row[0:1, :], in_=wa.unsqueeze(0))

        load_h(0, 0, 1)
        load_h(0, 1, 2)
        load_h(0, 2, 4)
        load_scales(wv_plane, wv_scales)
        load_codes(wv_codes, wv_words, 0, PASSES)
        load_h(1, 0, 2)
        load_h(1, 2, 4)
        load_scales(wu_plane, wu_scales)
        load_codes(wu_codes, wu_words, 0, PASSES)
        for b in range(2, B):
            load_h(b, 0, 2)
            load_h(b, 2, 4)
        load_scales(w1_plane, w1_scales)
        load_codes(w1_codes, w1_words, 0, 1)
        load_codes(w1_codes, w1_words, 1, 2)
        b1_all = keep.tile([P, PASSES, BANK], BF16)
        nc.sync.dma_start(out=b1_all[:].rearrange("p g f -> p (g f)"), in_=b1.partition_broadcast(P))
        load_scales(w2_plane, w2_scales)
        load_codes(w2_codes, w2_words, 0, PASSES)

        wa_all = keep.tile([P, A], F32)
        h_codes = [keep.tile([P, 2, PASSES * P], U32, name="h_codes%d" % j, align_bytes=64) for j in range(PAIRS)]
        h_scales = [keep.tile([P, 2, PASSES * P], U8, name="h_scales%d" % j, align_bytes=64) for j in range(PAIRS)]
        neg_e = [keep.tile([P, 2, PACK], F32, name="neg_e%d" % k) for k in range(B // 2)]
        row_min = [keep.tile([P, 2], F32, name="row_min%d" % k) for k in range(B // 2)]
        bag_min = [keep.tile([P, 2], F32, name="bag_min%d" % k) for k in range(B // 2)]
        row_sum = [keep.tile([P, 2], F32, name="row_sum%d" % k) for k in range(B // 2)]
        inverse = [keep.tile([P, 2], F32, name="inverse%d" % k) for k in range(B // 2)]
        expo = [keep.tile([P, PACK], F32, name="expo%d" % b) for b in range(B)]
        attn = [keep.tile([P, PACK], F32, name="attn%d" % b) for b in range(B)]
        out_codes = keep.tile([P, B * C], U32, align_bytes=64)
        out_scales = keep.tile([P, B * C], U8, align_bytes=64)

        def spread_wa(index):
            bank = next_bank()
            nc.tensor.matmul(bank[:, 0:A], lhsT=ones[:], rhs=wa_row[:], start=True, stop=True)
            held["wa_bank", index] = bank

        def halve_wa(index):
            nc.vector.tensor_scalar(
                out=wa_all[:], in0=held["wa_bank", index][:, 0:A], scalar1=-0.5, scalar2=None, op0=ALU.mult
            )

        def turn_h(i):
            words = h_raw[i // PACK][:, i % PACK, :].bitcast(F32)
            bank = next_bank()
            for u in range(2):
                for g in range(PASSES):
                    col = (u * PASSES + g) * P
                    nc.tensor.transpose(bank[:, col : col + P], words[:, 256 * g + u : 256 * (g + 1) : 2], ident[:])
            held["h_bank", i] = bank

        def copy_h(i):
            if ("h_grouped", i // 2) not in held:
                held["h_grouped", i // 2] = work.tile([P, 2, D], BF16, name="h_grouped", align_bytes=64)
            dst = held["h_grouped", i // 2][:, i % 2, :].bitcast(F32).rearrange("p (q u) -> p q u", u=2)
            src = held["h_bank", i][:].rearrange("p (u q) -> p q u", u=2)
            if i in COPY_H_ON_VECTOR:
                nc.vector.tensor_copy(out=dst, in_=src)
            else:
                nc.scalar.copy(out=dst, in_=src)

        def quantise_h(j):
            nc.vector.quantize_mx(
                out=h_codes[j][:].rearrange("p s q -> p (s q)").bitcast(FP8X4),
                scales=h_scales[j][:].rearrange("p s q -> p (s q)"),
                in_=held["h_grouped", j][:].rearrange("p s d -> p (s d)"),
            )

        def times_h(out, i, codes, scales, cols):
            for g in range(PASSES):
                patches = slice(g * P, (g + 1) * P)
                nc.tensor.matmul_mx(
                    out=out, lhsT=h_codes[i // 2][:, i % 2, patches].bitcast(FP8X4),
                    lhsT_scale=h_scales[i // 2][:, i % 2, patches],
                    rhs=codes[:, g, cols].bitcast(FP8X4), rhs_scale=scales[:, g, cols],
                    start=(g == 0), stop=(g == PASSES - 1),
                )

        def gate_matmul(j, key, codes, scales):
            bank = next_bank()
            for s in range(2):
                times_h(bank[:, s * A : (s + 1) * A], 2 * j + s, codes, scales, slice(0, A))
            held[key, j] = bank

        def matmul_u(j):
            gate_matmul(j, "u_bank", wu_codes, wu_plane)

        def matmul_v(j):
            gate_matmul(j, "v_bank", wv_codes, wv_plane)

        def tanh_u(j):
            half_u = work.tile([P, 2, A], F32, name="tanh_u")
            nc.scalar.activation(
                out=half_u[:].rearrange("p s a -> p (s a)"), in_=held["u_bank", j][:], func=ACT.Tanh, scale=0.5
            )
            held["tanh_u", j] = half_u

        def tanh_v(j):
            whole_v = work.tile([P, 2, A], F32, name="tanh_v")
            nc.scalar.activation(out=whole_v[:].rearrange("p s a -> p (s a)"), in_=held["v_bank", j][:], func=ACT.Tanh)
            held["tanh_v", j] = whole_v

        def weigh_v(j):
            weighed = work.tile([P, 2, A], F32, name="weighed")
            engine = nc.gpsimd if j in WEIGH_ON_GPSIMD else nc.vector
            engine.tensor_tensor(
                out=weighed[:], in0=held["tanh_v", j][:], in1=wa_all[:].unsqueeze(1).to_broadcast([P, 2, A]), op=ALU.mult
            )
            held["weighed", j] = weighed

        def score(i):
            terms = work.tile([P, A], F32, name="terms")
            b, t = divmod(i, PACK)
            nc.vector.scalar_tensor_tensor(
                out=terms[:], in0=held["tanh_u", i // 2][:, i % 2, :], scalar=1.0,
                in1=held["weighed", i // 2][:, i % 2, :], op0=ALU.add, op1=ALU.mult,
                accum_out=neg_e[b // 2][:, b % 2, t : t + 1],
            )

        def min_rows(k):
            nc.vector.tensor_reduce(out=row_min[k][:], in_=neg_e[k][:], axis=AXIS.X, op=ALU.min)

        def spread_min(k):
            bank = next_bank()
            for s in range(2):
                nc.tensor.transpose(bank[:, s * P : (s + 1) * P], row_min[k][:, s : s + 1].to_broadcast([P, P]), ident[:])
            held["min_bank", k] = bank

        def min_bags(k):
            spread = held["min_bank", k][:, 0 : 2 * P].rearrange("p (s n) -> p s n", s=2)
            nc.vector.tensor_reduce(out=bag_min[k][:], in_=spread, axis=AXIS.X, op=ALU.min)

        def exponent(b):
            k, s = divmod(b, 2)
            nc.scalar.activation(
                out=expo[b][:], in_=neg_e[k][:, s, :], func=ACT.Exp, scale=-1.0, bias=bag_min[k][:, s : s + 1],
                accum_out=row_sum[k][:, s : s + 1],
            )

        def mean_bags(k):
            bank = next_bank()
            nc.tensor.matmul(bank[:, 0:2], lhsT=per_patch[:], rhs=row_sum[k][:], start=True, stop=True)
            held["mean_bank", k] = bank

        def invert(k):
            nc.vector.reciprocal(out=inverse[k][:], in_=held["mean_bank", k][:, 0:2])

        def normalise(b):
            k, s = divmod(b, 2)
            nc.scalar.activation(out=attn[b][:], in_=expo[b][:], func=ACT.Copy, scale=inverse[k][:, s : s + 1])

        def matmul_z(n):
            i, g = divmod(n, PASSES)
            bank = next_bank()
            times_h(bank[:], i, w1_codes, w1_plane, slice(g * BANK, (g + 1) * BANK))
            held["z_bank", n] = bank

        def affine(n):
            i, g = divmod(n, PASSES)
            if g == 0:
                held["pre", i] = work.tile([P, PASSES, BANK], BF16, name="pre", bufs=PRE_BUFS)
            b, t = divmod(i, PACK)
            z, bias, pre = held["z_bank", n][:], b1_all[:, g, :], held["pre", i][:, g, :]
            if i in STEPPED_TURN:
                parts = [(z, bias, pre)]
            else:
                z, bias = [x.rearrange("p (m u e) -> p u m e", u=2, e=2) for x in (z, bias)]
                pre = pre.rearrange("p (u m e) -> p u m e", u=2, e=2)
                parts = [(z[:, u], bias[:, u], pre[:, u]) for u in range(2)]
            for z_part, bias_part, pre_part in parts:
                nc.vector.scalar_tensor_tensor(
                    out=pre_part, in0=z_part, scalar=attn[b][:, t : t + 1], in1=bias_part, op0=ALU.mult, op1=ALU.add
                )

        def turn_passes(i, passes):
            words = held["pre", i][:].rearrange("p g f -> p (g f)").bitcast(F32)
            bank = next_bank()
            for place, g in enumerate(passes):
                for u in range(2):
                    col = (u * len(passes) + place) * P
                    if i in STEPPED_TURN:
                        src = words[:, 256 * g + u : 256 * (g + 1) : 2]
                    else:
                        src = words[:, (g * 2 + u) * P : (g * 2 + u + 1) * P]
                    nc.tensor.transpose(bank[:, col : col + P], src, ident[:])
            held["p_bank", i, passes[0]] = bank

        def turn_p(i):
            turn_passes(i, (0, 1))

        def turn_last(g):
            turn_passes(LAST, (g,))

        def relu_passes(i, first, count, on_vector):
            if ("p_grouped", i // 2) not in held:
                held["p_grouped", i // 2] = work.tile([P, 2, F], BF16, name="p_grouped", align_bytes=64)
            cols = slice(first * BANK, (first + count) * BANK)
            dst = held["p_grouped", i // 2][:, i % 2, cols].rearrange("p (q u e) -> p q u e", u=2, e=2)
            values = held["p_bank", i, first][:].bitcast(BF16)[:, 0 : count * BANK]
            src = values.rearrange("p (u q e) -> p q u e", u=2, e=2)
            if on_vector:
                nc.vector.tensor_scalar(out=dst, in0=src, scalar1=0.0, scalar2=None, op0=ALU.max)
            else:
                nc.scalar.activation(out=dst, in_=src, func=ACT.Relu)

        def relu_p(i):
            relu_passes(i, 0, PASSES, on_vector=False)

        def relu_last(g):
            relu_passes(LAST, g, 1, on_vector=True)

        def quantise_passes(j, first, count):
            if first == 0:
                codes = work.tile([P, 2 * PASSES * P], U32, name="p_codes", align_bytes=64, bufs=PRE_BUFS)
                scales = work.tile([P, 2 * PASSES * P], U8, name="p_scales", align_bytes=64, bufs=PRE_BUFS)
                held["p_quantised", j] = (codes, scales)
            codes, scales = held["p_quantised", j]
            cols = slice(first * P, (first + count) * P)
            src = held["p_grouped", j][:].rearrange("p s f -> p (s f)")[:, first * BANK : (first + count) * BANK]
            nc.vector.quantize_mx(out=codes[:, cols].bitcast(FP8X4), scales=scales[:, cols], in_=src)

        def quantise_p(j):
            quantise_passes(j, 0, 2 * PASSES if j < PAIRS - 1 else PASSES)

        def quantise_last(g):
            quantise_passes(PAIRS - 1, PASSES + g, 1)

        def out_pass(out, i, g):
            codes, scales = held["p_quantised", i // 2]
            place = PASSES * (i % 2) + g
            patches = slice(place * P, (place + 1) * P)
            nc.tensor.matmul_mx(
                out=out, lhsT=codes[:, patches].bitcast(FP8X4), lhsT_scale=scales[:, patches],
                rhs=w2_codes[:, g, :].bitcast(FP8X4), rhs_scale=w2_plane[:, g, :],
                start=(g == 0), stop=(g == PASSES - 1),
            )

        def matmul_out(i):
            b, t = divmod(i, PACK)
            if t == 0:
                held["out_bank", b] = next_bank()
            for g in range(PASSES):
                out_pass(held["out_bank", b][:, t * C : (t + 1) * C], i, g)

        def matmul_last(g):
            if g == 0:
                held["last_bank"] = next_bank()
            out_pass(held["last_bank"][:, 0:C], LAST, g)

        def store_tiles(b, src, t0, t1):
            if ("result", b) not in held:
                held["result", b] = work.tile([P, PACK * C], F32, name="result")
            cols = slice(t0 * C, t1 * C)
            nc.scalar.copy(out=held["result", b][:, cols], in_=src)
            nc.sync.dma_start(out=out_0[b].rearrange("(p t) c -> p (t c)", t=PACK)[:, cols], in_=held["result", b][:, cols])

        def store_out(b):
            tiles = PACK if b < B - 1 else PACK - 1
            store_tiles(b, held["out_bank", b][:, 0 : tiles * C], 0, tiles)

        def store_last(b):
            store_tiles(b, held["last_bank"][:, 0:C], PACK - 1, PACK)

        def round_out(b):
            grouped = work.tile([P, C, PACK], BF16, name="out_grouped", align_bytes=64)
            if b in ROUND_ON_VECTOR:
                nc.vector.tensor_copy(out=grouped[:], in_=held["result", b][:].rearrange("p (t c) -> p c t", t=PACK))
            else:
                nc.scalar.copy(out=grouped[:], in_=held["out_bank", b][:].rearrange("p (t c) -> p c t", t=PACK))
            held["out_grouped", b] = grouped

        def quantise_out(b):
            cols = slice(b * C, (b + 1) * C)
            nc.vector.quantize_mx(
                out=out_codes[:, cols].bitcast(FP8X4), scales=out_scales[:, cols],
                in_=held["out_grouped", b][:].rearrange("p c t -> p (c t)"),
            )
            nc.sync.dma_start(
                out=out_1[0].rearrange("p m t -> p (m t)").bitcast(I32)[:, cols], in_=out_codes[:, cols].bitcast(I32)
            )

        steps = {
            "spread_wa": spread_wa, "halve_wa": halve_wa,
            "turn_h": turn_h, "copy_h": copy_h, "quantise_h": quantise_h,
            "matmul_u": matmul_u, "matmul_v": matmul_v, "tanh_u": tanh_u, "tanh_v": tanh_v,
            "weigh_v": weigh_v, "score": score,
            "min_rows": min_rows, "spread_min": spread_min, "min_bags": min_bags, "exponent": exponent,
            "mean_bags": mean_bags, "invert": invert, "normalise": normalise,
            "matmul_z": matmul_z, "affine": affine,
            "turn_p": turn_p, "relu_p": relu_p, "quantise_p": quantise_p, "matmul_out": matmul_out,
            "turn_last": turn_last, "relu_last": relu_last, "quantise_last": quantise_last, "matmul_last": matmul_last,
            "store_out": store_out, "store_last": store_last, "round_out": round_out, "quantise_out": quantise_out,
        }
        for entry in ORDER.split():
            step, index = entry.split(":")
            steps[step](int(index))

        for quad in range(4):
            queue = nc.sync if quad % 2 == 0 else nc.scalar
            queue.dma_start(
                out=out_2[0, 4 * quad : 4 * quad + 4, :].bitcast(I32),
                in_=out_scales[32 * quad : 32 * quad + 4, :].bitcast(I32),
            )
